import numpy as np
import ml_dtypes


def mxq(x, axis, fmt="e4m3"):
    dtype, down = {"e4m3": (ml_dtypes.float8_e4m3fn, 7), "e5m2": (ml_dtypes.float8_e5m2, 14)}[fmt]
    v = np.moveaxis(np.asarray(x, np.float32).astype(ml_dtypes.bfloat16).astype(np.float64), axis, -1)
    blocks = v.reshape(v.shape[:-1] + (-1, 32))
    amax = np.abs(blocks).max(-1, keepdims=True)
    byte = np.maximum(np.where(amax > 0, np.frexp(amax)[1] - 1 + 127, 0) - down, 1)
    scale = np.exp2(byte - 127.0)
    codes = (blocks / scale).astype(np.float32).astype(dtype).astype(np.float64)
    return np.moveaxis((codes * scale).reshape(v.shape), -1, axis)


WIDE = False


def mx_kscale(k):
    if not WIDE:
        return np.ones(k)
    levels = np.array([10, -10, 5, -5, 0])
    if k % 512:
        return np.exp2(np.random.permutation(np.resize(levels, k // 32))).repeat(32)
    a = np.empty((k // 512, 16))
    for p in range(k // 512):
        a[p, :8] = np.random.permutation(np.resize(levels, 8))
        for g in range(8):
            far = levels[np.abs(levels - a[p, g]) >= 10]
            a[p, g + 8] = far[np.random.randint(len(far))]
    return np.exp2(a.ravel()).repeat(32)


BF16 = ml_dtypes.bfloat16


def bf(x):
    return np.asarray(x, np.float32).astype(BF16)


def f64(x):
    return np.asarray(x).astype(np.float64)


M, N, R = 1536, 1024, 512
LEAK, COUPLING, DRIVE = 0.8, 0.35, 0.2


def draw0():
    s = mx_kscale(N)
    x = np.random.standard_normal((M, N))
    w = COUPLING * np.random.standard_normal((N, N)) / np.sqrt(N)
    a = LEAK + 0.05 * np.random.standard_normal(N)
    d = DRIVE * np.random.standard_normal(N)
    c = np.random.standard_normal((N, R)) / np.sqrt(N)
    return {"x": bf(x * s),
            "w": bf(w / s[:, None] * s),
            "a": bf(a),
            "d": bf(d * s),
            "c": bf(c / s[:, None])}


def core(x, w, a, d, c):
    x0, keep, drive = f64(x), f64(a), f64(d)
    wq = mxq(f64(w), 0, "e4m3")
    x1 = keep * x0 + (mxq(x0, 1, "e4m3") @ wq) + drive
    x2 = keep * x1 + (mxq(x1, 1, "e4m3") @ wq) + drive
    y = mxq(x2, 1, "e4m3") @ mxq(f64(c), 0, "e4m3")
    return y


def e4m3fn_bytes(y):
    return np.clip(np.asarray(y, np.float64), -448.0, 448.0).astype(np.float32).astype(ml_dtypes.float8_e4m3fn).view(np.uint8)


def e4m3fn_values(b):
    return np.asarray(b, np.uint8).view(ml_dtypes.float8_e4m3fn).astype(np.float64)


def setup_inputs():
    d = draw0()
    x0 = np.asarray(d['c']).astype(np.float64)
    s = (np.max(np.abs(x0), axis=(1,), keepdims=True) / 448.0).astype(np.float32)
    out = {}
    for k, v in d.items():
        if k == 'c':
            out['c_bytes'] = e4m3fn_bytes(x0 / s.astype(np.float64))
            out['c_scale'] = s
        else:
            out[k] = v
    return out


def reference(x, w, a, d, c_bytes, c_scale):
    return core(x, w, a, d, e4m3fn_values(c_bytes) * c_scale.astype(np.float64))

@@ -1,0 +1,363 @@
+from contextlib import ExitStack
+
+import concourse.mybir as mybir
+from concourse.masks import make_identity
+
+M, N, R = 1536, 1024, 512
+FLOPS = 2 * M * N * (N + N + R)
+
+P = 128
+ROWS = 256
+CHUNKS = M // ROWS
+
+F32 = mybir.dt.float32
+BF16 = mybir.dt.bfloat16
+U32 = mybir.dt.uint32
+U8 = mybir.dt.uint8
+FP8 = mybir.dt.float8_e4m3fn
+FP8X4 = mybir.dt.float8_e4m3fn_x4
+ADD = mybir.AluOpType.add
+MULT = mybir.AluOpType.mult
+IDENT = mybir.ActivationFunctionType.Identity
+COPY = mybir.ActivationFunctionType.Copy
+
+
+def tile_hopfield_euler_readout_t1_kernel(tc, x, w, a, d, c_bytes, c_scale, out):
+    nc = tc.nc
+    with ExitStack() as ctx:
+        keep = ctx.enter_context(tc.tile_pool(name="keep", bufs=1))
+        xin = ctx.enter_context(tc.tile_pool(name="xin", bufs=6))
+        work = ctx.enter_context(tc.tile_pool(name="work", bufs=3))
+        two = ctx.enter_context(tc.tile_pool(name="two", bufs=2))
+        ps_mm = ctx.enter_context(tc.psum_pool(name="ps_mm", bufs=4))
+        ps_xt = ctx.enter_context(tc.psum_pool(name="ps_xt", bufs=2))
+        ps_y = ctx.enter_context(tc.psum_pool(name="ps_y", bufs=2))
+
+        a_bf = keep.tile([P, 2, 4], BF16)
+        d_bf = keep.tile([P, 2, 4], BF16)
+        c_sc = keep.tile([P, 2, 4], F32)
+        nc.scalar.dma_start(out=a_bf[:], in_=a.rearrange("(g p t) -> p g t", p=P, t=4))
+        nc.scalar.dma_start(out=d_bf[:], in_=d.rearrange("(g p t) -> p g t", p=P, t=4))
+
+        ident = keep.tile([P, P], F32)
+        make_identity(nc, ident[:])
+
+        x_tiles = {}
+
+        def load_x(i, hs=(0, 1)):
+            for h in hs:
+                x_sb = xin.tile([P, N], BF16, name="x_sb")
+                r0 = i * ROWS + h * P
+                nc.sync.dma_start(out=x_sb[:], in_=x[r0 : r0 + P, :])
+                x_tiles[(i, h)] = x_sb
+
+        w_view = w.rearrange("(g p j) c -> g p j c", p=P, j=4)
+        w_raw = {}
+
+        def load_w(go, g):
+            if g == 0:
+                w_sb = keep.tile([P, 2, 4, 512], BF16, name="w_raw%d" % go)
+                w_raw[go] = w_sb
+            if True:
+                nc.sync.dma_start(out=w_raw[go][:, g], in_=w_view[g][:, :, go * 512 : go * 512 + 512])
+
+        c_by = keep.tile([P, 2, 4, R], U8, align_bytes=64)
+
+        with tc.manual_schedule():
+            warm = keep.tile([P, 1], F32)
+            nc.vector.memset(warm[:], 0.0)
+            warm2 = keep.tile([P, 1], F32)
+            nc.scalar.activation(warm2[:], warm[:], IDENT)
+
+            load_x(0, (0,))
+            load_w(0, 0)
+            load_w(0, 1)
+            load_x(0, (1,))
+            load_w(1, 0)
+            load_w(1, 1)
+            load_x(1)
+            nc.sync.dma_start(out=c_by[:], in_=c_bytes.rearrange("(g p j) r -> p g j r", p=P, j=4))
+            nc.scalar.dma_start(out=c_sc[:], in_=c_scale.rearrange("(g p j) o -> p g (j o)", p=P, j=4))
+            load_x(2)
+
+            a_f = keep.tile([P, 2, 4], F32)
+            d_f = keep.tile([P, 2, 4], F32)
+            nc.vector.tensor_copy(out=a_f[:], in_=a_bf[:])
+            nc.vector.tensor_copy(out=d_f[:], in_=d_bf[:])
+
+            def a_col(n):
+                return a_f[:, n // 4, n % 4 : n % 4 + 1]
+
+            def d_col(n):
+                return d_f[:, n // 4, n % 4 : n % 4 + 1]
+
+            xt_ps, xg, xc, xs, t1, x1f, x1b, x1c, x1s, t2, x2b, x2c, x2s = ({} for _ in range(13))
+            wc, ws, wg = {}, {}, {}
+            cw, cg, cc, cs = {}, {}, {}, {}
+            s1, s2, y_ps = {}, {}, {}
+
+            def T(i, hs=(0, 1)):
+                for h in hs:
+                    xt = ps_xt.tile([P, 2, 2, P], F32, name="xt")
+                    words = x_tiles[(i, h)][:].bitcast(F32)
+                    for g in range(2):
+                        for u in range(2):
+                            nc.tensor.transpose(xt[:, g, u, :], words[:, 256 * g + u : 256 * g + 256 : 2], ident[:])
+                    xt_ps[(i, h)] = xt
+
+            def XO(i, hs=(0, 1)):
+                if 0 in hs:
+                    xg_t = work.tile([P, 2, ROWS, 2], F32, name="xg_t", align_bytes=64)
+                    xg[i] = xg_t
+                for h in hs:
+                    nc.scalar.copy(
+                        out=xg[i][:, :, h * P : h * P + P, :], in_=xt_ps[(i, h)][:].rearrange("p g u r -> p g r u")
+                    )
+
+            def QX(i):
+                xc_t = work.tile([P, 2, ROWS], U32, name="xc_t", align_bytes=64)
+                xs_t = work.tile([P, 2, ROWS], U8, name="xs_t", align_bytes=64)
+                xc[i], xs[i] = xc_t, xs_t
+                nc.vector.quantize_mx(
+                    out=xc_t[:].rearrange("p g r -> p (g r)").bitcast(FP8X4),
+                    scales=xs_t[:].rearrange("p g r -> p (g r)"),
+                    in_=xg[i][:].rearrange("p g r u -> p (g r u)").bitcast(BF16),
+                )
+
+            def TMP1(i):
+                t1_t = two.tile([P, 8, ROWS], F32, name="t1_t")
+                t1[i] = t1_t
+                xv = xg[i][:].rearrange("p g r u -> p (g r u)").bitcast(BF16).rearrange("p (g r t) -> p g r t", g=2, t=4)
+                for n in range(8):
+                    nc.gpsimd.tensor_scalar(
+                        out=t1_t[:, n, :], in0=xv[:, n // 4, :, n % 4], scalar1=a_col(n), scalar2=d_col(n), op0=MULT, op1=ADD
+                    )
+
+            def S1(i, go):
+                for h in range(2):
+                    mm = ps_mm.tile([P, 2, ROWS], F32, name="mm")
+                    for tt in range(2):
+                        t = 2 * h + tt
+                        for g in range(2):
+                            nc.tensor.matmul_mx(
+                                out=mm[:, tt, :],
+                                lhsT=wc[go][:, g, t * P : t * P + P].bitcast(FP8X4),
+                                lhsT_scale=ws[go][:, g, t * P : t * P + P],
+                                rhs=xc[i][:, g, :].bitcast(FP8X4),
+                                rhs_scale=xs[i][:, g, :],
+                                start=(g == 0),
+                                stop=(g == 1),
+                            )
+                    s1[(i, go, h)] = mm
+
+            def A1(i, go):
+                if go == 0:
+                    x1f_t = two.tile([P, 8, ROWS], F32, name="x1f_t")
+                    x1f[i] = x1f_t
+                for h in range(2):
+                    n = 4 * go + 2 * h
+                    nc.vector.tensor_tensor(
+                        out=x1f[i][:, n : n + 2, :], in0=s1[(i, go, h)][:], in1=t1[i][:, n : n + 2, :], op=ADD
+                    )
+
+            def IL(i):
+                x1b_t = two.tile([P, 2, ROWS, 4], BF16, name="x1b_t", align_bytes=64)
+                x1b[i] = x1b_t
+                for go in range(2):
+                    nc.scalar.copy(out=x1b_t[:, go], in_=x1f[i][:, 4 * go : 4 * go + 4, :].rearrange("p t r -> p r t"))
+
+            def QX1(i):
+                x1c_t = two.tile([P, 2, ROWS], U32, name="x1c_t", align_bytes=64)
+                x1s_t = two.tile([P, 2, ROWS], U8, name="x1s_t", align_bytes=64)
+                x1c[i], x1s[i] = x1c_t, x1s_t
+                nc.vector.quantize_mx(
+                    out=x1c_t[:].rearrange("p g r -> p (g r)").bitcast(FP8X4),
+                    scales=x1s_t[:].rearrange("p g r -> p (g r)"),
+                    in_=x1b[i][:].rearrange("p g r t -> p (g r t)"),
+                )
+
+            def TMP2(i):
+                t2_t = two.tile([P, 8, ROWS], F32, name="t2_t")
+                t2[i] = t2_t
+                for n in range(8):
+                    if n in (7,):
+                        nc.gpsimd.tensor_scalar(
+                            out=t2_t[:, n, :], in0=x1f[i][:, n, :], scalar1=a_col(n), scalar2=d_col(n), op0=MULT, op1=ADD
+                        )
+                    else:
+                        nc.scalar.activation(t2_t[:, n, :], x1f[i][:, n, :], IDENT, bias=d_col(n), scale=a_col(n))
+
+            def S2(i):
+                for h in range(2):
+                    for go in range(2):
+                        mm = ps_mm.tile([P, 4, P], F32, name="mm")
+                        for t in range(4):
+                            for g in range(2):
+                                nc.tensor.matmul_mx(
+                                    out=mm[:, t, :],
+                                    lhsT=wc[go][:, g, t * P : t * P + P].bitcast(FP8X4),
+                                    lhsT_scale=ws[go][:, g, t * P : t * P + P],
+                                    rhs=x1c[i][:, g, h * P : h * P + P].bitcast(FP8X4),
+                                    rhs_scale=x1s[i][:, g, h * P : h * P + P],
+                                    start=(g == 0),
+                                    stop=(g == 1),
+                                )
+                        s2[(i, go, h)] = mm
+
+            def A2(i, h):
+                if h == 0:
+                    x2b_t = two.tile([P, 2, 2, P, 4], BF16, name="x2b_t", align_bytes=64)
+                    x2b[i] = x2b_t
+                if True:
+                    for go in range(2):
+                        rs = slice(h * P, h * P + P)
+                        nc.vector.tensor_tensor(
+                            out=x2b[i][:, h, go],
+                            in0=s2[(i, go, h)][:].rearrange("p t r -> p r t"),
+                            in1=t2[i][:, 4 * go : 4 * go + 4, rs].rearrange("p t r -> p r t"),
+                            op=ADD,
+                        )
+
+            def QX2(i, h):
+                x2c_t = two.tile([P, 2, P], U32, name="x2c_t%d" % h, align_bytes=64)
+                x2s_t = two.tile([P, 2, P], U8, name="x2s_t%d" % h, align_bytes=64)
+                x2c[(i, h)], x2s[(i, h)] = x2c_t, x2s_t
+                nc.vector.quantize_mx(
+                    out=x2c_t[:].rearrange("p g r -> p (g r)").bitcast(FP8X4),
+                    scales=x2s_t[:].rearrange("p g r -> p (g r)"),
+                    in_=x2b[i][:, h].rearrange("p g r t -> p (g r t)"),
+                )
+
+            def S3(i):
+                for h in range(2):
+                    yp = ps_y.tile([P, R], F32, name="yp")
+                    for g in range(2):
+                        nc.tensor.matmul_mx(
+                            out=yp[:],
+                            lhsT=x2c[(i, h)][:, g, :].bitcast(FP8X4),
+                            lhsT_scale=x2s[(i, h)][:, g, :],
+                            rhs=cc[0][:, g, :].bitcast(FP8X4),
+                            rhs_scale=cs[0][:, g, :],
+                            start=(g == 0),
+                            stop=(g == 1),
+                        )
+                    y_ps[(i, h)] = yp
+
+            def YO(i):
+                for h in range(2):
+                    y_sb = work.tile([P, R], F32, name="y_sb")
+                    nc.scalar.copy(out=y_sb[:], in_=y_ps[(i, h)][:])
+                    r0 = i * ROWS + h * P
+                    nc.sync.dma_start(out=out[r0 : r0 + P, :], in_=y_sb[:])
+
+            def WI(go, g, eng, t0=0, t1_=4):
+                if go not in wg:
+                    wg_t = keep.tile([P, 2, 512, 4], BF16, name="wg%d" % go, align_bytes=64)
+                    wg[go] = wg_t
+                o = wg[go][:, g].rearrange("p (t m) j -> p t m j", t=4)[:, t0:t1_]
+                i_ = w_raw[go][:, g].rearrange("p j (m t) -> p t m j", t=4)[:, t0:t1_]
+                if eng == "v":
+                    nc.vector.tensor_copy(out=o, in_=i_)
+                else:
+                    nc.scalar.copy(out=o, in_=i_)
+
+            def WQ(go):
+                wc_t = keep.tile([P, 2, 512], U32, name="wc%d" % go, align_bytes=64)
+                ws_t = keep.tile([P, 2, 512], U8, name="ws%d" % go, align_bytes=64)
+                wc[go], ws[go] = wc_t, ws_t
+                nc.vector.quantize_mx(
+                    out=wc_t[:].rearrange("p g c -> p (g c)").bitcast(FP8X4),
+                    scales=ws_t[:].rearrange("p g c -> p (g c)"),
+                    in_=wg[go][:].rearrange("p g c j -> p (g c j)"),
+                )
+
+            def CW(g):
+                cw_t = keep.tile([P, 4, R], BF16, name="cw%d" % g)
+                cw[g] = cw_t
+                for j in range(4):
+                    nc.vector.tensor_scalar(
+                        out=cw_t[:, j, :], in0=c_by[:, g, j, :].bitcast(FP8), scalar1=c_sc[:, g, j : j + 1], scalar2=None, op0=MULT
+                    )
+
+            def CI(g):
+                if 0 not in cg:
+                    cg_t = keep.tile([P, 2, R, 4], BF16, name="cg", align_bytes=64)
+                    cg[0] = cg_t
+                nc.gpsimd.tensor_scalar(
+                    out=cg[0][:, g], in0=cw[g][:].rearrange("p j r -> p r j"), scalar1=1.0, scalar2=0.0, op0=MULT, op1=ADD
+                )
+
+            def CQ():
+                cc_t = keep.tile([P, 2, R], U32, name="cc", align_bytes=64)
+                cs_t = keep.tile([P, 2, R], U8, name="cs", align_bytes=64)
+                cc[0], cs[0] = cc_t, cs_t
+                nc.vector.quantize_mx(
+                    out=cc_t[:].rearrange("p g r -> p (g r)").bitcast(FP8X4),
+                    scales=cs_t[:].rearrange("p g r -> p (g r)"),
+                    in_=cg[0][:].rearrange("p g r j -> p (g r j)"),
+                )
+
+            T(0, (0,))
+            XO(0, (0,))
+            WI(0, 0, "v")
+            WI(0, 1, "s", 2, 4)
+            WI(0, 1, "v", 0, 2)
+            T(0, (1,))
+            XO(0, (1,))
+            WQ(0)
+            QX(0)
+            TMP1(0)
+            WI(1, 0, "v")
+            WI(1, 1, "s")
+            S1(0, 0)
+            A1(0, 0)
+            T(1)
+            XO(1)
+            WQ(1)
+            S1(0, 1)
+            QX(1)
+            TMP1(1)
+            A1(0, 1)
+            IL(0)
+            T(2)
+            XO(2)
+            CW(0)
+            CW(1)
+            CI(0)
+            CI(1)
+            QX1(0)
+            for i in range(CHUNKS + 1):
+                if i + 3 < CHUNKS:
+                    load_x(i + 3)
+                if i + 1 < CHUNKS:
+                    S1(i + 1, 0)
+                    S1(i + 1, 1)
+                if i < CHUNKS:
+                    TMP2(i)
+                if i + 1 < CHUNKS:
+                    A1(i + 1, 0)
+                    A1(i + 1, 1)
+                if i < CHUNKS:
+                    S2(i)
+                if i == 1:
+                    CQ()
+                if i >= 1:
+                    S3(i - 1)
+                if i + 1 < CHUNKS:
+                    IL(i + 1)
+                if i >= 1:
+                    YO(i - 1)
+                if i + 2 < CHUNKS:
+                    QX(i + 2)
+                    TMP1(i + 2)
+                if i + 3 < CHUNKS:
+                    T(i + 3)
+                    XO(i + 3)
+                if i < CHUNKS:
+                    A2(i, 0)
+                    A2(i, 1)
+                if i + 1 < CHUNKS:
+                    QX1(i + 1)
+                if i < CHUNKS:
+                    QX2(i, 0)
+                    QX2(i, 1)

@@ -22,6 +22,9 @@ IDENT = mybir.ActivationFunctionType.Identity
 COPY = mybir.ActivationFunctionType.Copy
 
 
+V2 = {0: (3, 7), 5: (1, 3, 5, 7)}
+
+
 def tile_hopfield_euler_readout_t1_kernel(tc, x, w, a, d, c_bytes, c_scale, out):
     nc = tc.nc
     with ExitStack() as ctx:
@@ -124,11 +127,11 @@ def tile_hopfield_euler_readout_t1_kernel(tc, x, w, a, d, c_bytes, c_scale, out)
                     in_=xg[i][:].rearrange("p g r u -> p (g r u)").bitcast(BF16),
                 )
 
-            def TMP1(i):
-                t1_t = two.tile([P, 8, ROWS], F32, name="t1_t")
-                t1[i] = t1_t
+            t1_t = keep.tile([P, 8, ROWS], F32)
+
+            def TMP1(i, gos=(0, 1)):
                 xv = xg[i][:].rearrange("p g r u -> p (g r u)").bitcast(BF16).rearrange("p (g r t) -> p g r t", g=2, t=4)
-                for n in range(8):
+                for n in range(4 * gos[0], 4 * gos[-1] + 4):
                     nc.gpsimd.tensor_scalar(
                         out=t1_t[:, n, :], in0=xv[:, n // 4, :, n % 4], scalar1=a_col(n), scalar2=d_col(n), op0=MULT, op1=ADD
                     )
@@ -157,14 +160,17 @@ def tile_hopfield_euler_readout_t1_kernel(tc, x, w, a, d, c_bytes, c_scale, out)
                 for h in range(2):
                     n = 4 * go + 2 * h
                     nc.vector.tensor_tensor(
-                        out=x1f[i][:, n : n + 2, :], in0=s1[(i, go, h)][:], in1=t1[i][:, n : n + 2, :], op=ADD
+                        out=x1f[i][:, n : n + 2, :], in0=t1_t[:, n : n + 2, :], in1=s1[(i, go, h)][:], op=ADD
                     )
 
             def IL(i):
                 x1b_t = two.tile([P, 2, ROWS, 4], BF16, name="x1b_t", align_bytes=64)
                 x1b[i] = x1b_t
                 for go in range(2):
-                    nc.scalar.copy(out=x1b_t[:, go], in_=x1f[i][:, 4 * go : 4 * go + 4, :].rearrange("p t r -> p r t"))
+                    nc.scalar.copy(
+                        out=x1b_t[:, go].rearrange("p (c i) t -> p c t i", i=4),
+                        in_=x1f[i][:, 4 * go : 4 * go + 4, :].rearrange("p t (c i) -> p c t i", i=4),
+                    )
 
             def QX1(i):
                 x1c_t = two.tile([P, 2, ROWS], U32, name="x1c_t", align_bytes=64)
@@ -180,8 +186,8 @@ def tile_hopfield_euler_readout_t1_kernel(tc, x, w, a, d, c_bytes, c_scale, out)
                 t2_t = two.tile([P, 8, ROWS], F32, name="t2_t")
                 t2[i] = t2_t
                 for n in range(8):
-                    if n in (7,):
-                        nc.gpsimd.tensor_scalar(
+                    if n in V2.get(i, ()):
+                        nc.vector.tensor_scalar(
                             out=t2_t[:, n, :], in0=x1f[i][:, n, :], scalar1=a_col(n), scalar2=d_col(n), op0=MULT, op1=ADD
                         )
                     else:
@@ -213,14 +219,14 @@ def tile_hopfield_euler_readout_t1_kernel(tc, x, w, a, d, c_bytes, c_scale, out)
                         rs = slice(h * P, h * P + P)
                         nc.vector.tensor_tensor(
                             out=x2b[i][:, h, go],
-                            in0=s2[(i, go, h)][:].rearrange("p t r -> p r t"),
-                            in1=t2[i][:, 4 * go : 4 * go + 4, rs].rearrange("p t r -> p r t"),
+                            in0=t2[i][:, 4 * go : 4 * go + 4, rs].rearrange("p t r -> p r t"),
+                            in1=s2[(i, go, h)][:].rearrange("p t r -> p r t"),
                             op=ADD,
                         )
 
             def QX2(i, h):
-                x2c_t = two.tile([P, 2, P], U32, name="x2c_t%d" % h, align_bytes=64)
-                x2s_t = two.tile([P, 2, P], U8, name="x2s_t%d" % h, align_bytes=64)
+                x2c_t = work.tile([P, 2, P], U32, name="x2c_t%d" % h, align_bytes=64)
+                x2s_t = work.tile([P, 2, P], U8, name="x2s_t%d" % h, align_bytes=64)
                 x2c[(i, h)], x2s[(i, h)] = x2c_t, x2s_t
                 nc.vector.quantize_mx(
                     out=x2c_t[:].rearrange("p g r -> p (g r)").bitcast(FP8X4),
@@ -245,7 +251,7 @@ def tile_hopfield_euler_readout_t1_kernel(tc, x, w, a, d, c_bytes, c_scale, out)
 
             def YO(i):
                 for h in range(2):
-                    y_sb = work.tile([P, R], F32, name="y_sb")
+                    y_sb = work.tile([P, R], F32, name="y_sb", bufs=6)
                     nc.scalar.copy(out=y_sb[:], in_=y_ps[(i, h)][:])
                     r0 = i * ROWS + h * P
                     nc.sync.dma_start(out=out[r0 : r0 + P, :], in_=y_sb[:])
@@ -283,9 +289,7 @@ def tile_hopfield_euler_readout_t1_kernel(tc, x, w, a, d, c_bytes, c_scale, out)
                 if 0 not in cg:
                     cg_t = keep.tile([P, 2, R, 4], BF16, name="cg", align_bytes=64)
                     cg[0] = cg_t
-                nc.gpsimd.tensor_scalar(
-                    out=cg[0][:, g], in0=cw[g][:].rearrange("p j r -> p r j"), scalar1=1.0, scalar2=0.0, op0=MULT, op1=ADD
-                )
+                nc.scalar.copy(out=cg[0][:, g], in_=cw[g][:].rearrange("p j r -> p r j"))
 
             def CQ():
                 cc_t = keep.tile([P, 2, R], U32, name="cc", align_bytes=64)
@@ -316,15 +320,12 @@ def tile_hopfield_euler_readout_t1_kernel(tc, x, w, a, d, c_bytes, c_scale, out)
             WQ(1)
             S1(0, 1)
             QX(1)
-            TMP1(1)
+            TMP1(1, (0,))
             A1(0, 1)
+            TMP1(1, (1,))
             IL(0)
             T(2)
             XO(2)
-            CW(0)
-            CW(1)
-            CI(0)
-            CI(1)
             QX1(0)
             for i in range(CHUNKS + 1):
                 if i + 3 < CHUNKS:
@@ -339,13 +340,16 @@ def tile_hopfield_euler_readout_t1_kernel(tc, x, w, a, d, c_bytes, c_scale, out)
                     A1(i + 1, 1)
                 if i < CHUNKS:
                     S2(i)
-                if i == 1:
+                if i == 2:
                     CQ()
-                if i >= 1:
+                    S3(0)
+                if i >= 2:
                     S3(i - 1)
                 if i + 1 < CHUNKS:
                     IL(i + 1)
-                if i >= 1:
+                if i == 2:
+                    YO(0)
+                if i >= 2:
                     YO(i - 1)
                 if i + 2 < CHUNKS:
                     QX(i + 2)
@@ -353,6 +357,9 @@ def tile_hopfield_euler_readout_t1_kernel(tc, x, w, a, d, c_bytes, c_scale, out)
                 if i + 3 < CHUNKS:
                     T(i + 3)
                     XO(i + 3)
+                if i < 2:
+                    CW(i)
+                    CI(i)
                 if i < CHUNKS:
                     A2(i, 0)
                     A2(i, 1)

@@ -22,7 +22,7 @@ IDENT = mybir.ActivationFunctionType.Identity
 COPY = mybir.ActivationFunctionType.Copy
 
 
-V2 = {0: (3, 7), 5: (1, 3, 5, 7)}
+V2 = {5: (3, 7)}
 
 
 def tile_hopfield_euler_readout_t1_kernel(tc, x, w, a, d, c_bytes, c_scale, out):
@@ -127,14 +127,18 @@ def tile_hopfield_euler_readout_t1_kernel(tc, x, w, a, d, c_bytes, c_scale, out)
                     in_=xg[i][:].rearrange("p g r u -> p (g r u)").bitcast(BF16),
                 )
 
-            t1_t = keep.tile([P, 8, ROWS], F32)
-
             def TMP1(i, gos=(0, 1)):
+                if 0 in gos:
+                    t1_t = two.tile([P, 8, ROWS], F32, name="t1_t")
+                    t1[i] = t1_t
                 xv = xg[i][:].rearrange("p g r u -> p (g r u)").bitcast(BF16).rearrange("p (g r t) -> p g r t", g=2, t=4)
                 for n in range(4 * gos[0], 4 * gos[-1] + 4):
-                    nc.gpsimd.tensor_scalar(
-                        out=t1_t[:, n, :], in0=xv[:, n // 4, :, n % 4], scalar1=a_col(n), scalar2=d_col(n), op0=MULT, op1=ADD
-                    )
+                    if i >= 2 and n == 7:
+                        nc.scalar.activation(t1[i][:, n, :], xv[:, n // 4, :, n % 4], IDENT, bias=d_col(n), scale=a_col(n))
+                    else:
+                        nc.vector.tensor_scalar(
+                            out=t1[i][:, n, :], in0=xv[:, n // 4, :, n % 4], scalar1=a_col(n), scalar2=d_col(n), op0=MULT, op1=ADD
+                        )
 
             def S1(i, go):
                 for h in range(2):
@@ -160,7 +164,7 @@ def tile_hopfield_euler_readout_t1_kernel(tc, x, w, a, d, c_bytes, c_scale, out)
                 for h in range(2):
                     n = 4 * go + 2 * h
                     nc.vector.tensor_tensor(
-                        out=x1f[i][:, n : n + 2, :], in0=t1_t[:, n : n + 2, :], in1=s1[(i, go, h)][:], op=ADD
+                        out=x1f[i][:, n : n + 2, :], in0=t1[i][:, n : n + 2, :], in1=s1[(i, go, h)][:], op=ADD
                     )
 
             def IL(i):
@@ -218,9 +222,9 @@ def tile_hopfield_euler_readout_t1_kernel(tc, x, w, a, d, c_bytes, c_scale, out)
                     for go in range(2):
                         rs = slice(h * P, h * P + P)
                         nc.vector.tensor_tensor(
-                            out=x2b[i][:, h, go],
-                            in0=t2[i][:, 4 * go : 4 * go + 4, rs].rearrange("p t r -> p r t"),
-                            in1=s2[(i, go, h)][:].rearrange("p t r -> p r t"),
+                            out=x2b[i][:, h, go].rearrange("p (c i) t -> p c t i", i=4),
+                            in0=t2[i][:, 4 * go : 4 * go + 4, rs].rearrange("p t (c i) -> p c t i", i=4),
+                            in1=s2[(i, go, h)][:].rearrange("p t (c i) -> p c t i", i=4),
                             op=ADD,
                         )
 
@@ -311,7 +315,8 @@ def tile_hopfield_euler_readout_t1_kernel(tc, x, w, a, d, c_bytes, c_scale, out)
             WQ(0)
             QX(0)
             TMP1(0)
-            WI(1, 0, "v")
+            WI(1, 0, "v", 0, 2)
+            WI(1, 0, "s", 2, 4)
             WI(1, 1, "s")
             S1(0, 0)
             A1(0, 0)
@@ -320,10 +325,9 @@ def tile_hopfield_euler_readout_t1_kernel(tc, x, w, a, d, c_bytes, c_scale, out)
             WQ(1)
             S1(0, 1)
             QX(1)
-            TMP1(1, (0,))
             A1(0, 1)
-            TMP1(1, (1,))
             IL(0)
+            TMP1(1)
             T(2)
             XO(2)
             QX1(0)

@@ -19,17 +19,14 @@ FP8X4 = mybir.dt.float8_e4m3fn_x4
 ADD = mybir.AluOpType.add
 MULT = mybir.AluOpType.mult
 IDENT = mybir.ActivationFunctionType.Identity
-COPY = mybir.ActivationFunctionType.Copy
-
-
-V2 = {5: (3, 7)}
+V2 = {5: (1, 3, 5, 7)}
+S1N = ()
 
 
 def tile_hopfield_euler_readout_t1_kernel(tc, x, w, a, d, c_bytes, c_scale, out):
     nc = tc.nc
     with ExitStack() as ctx:
         keep = ctx.enter_context(tc.tile_pool(name="keep", bufs=1))
-        xin = ctx.enter_context(tc.tile_pool(name="xin", bufs=6))
         work = ctx.enter_context(tc.tile_pool(name="work", bufs=3))
         two = ctx.enter_context(tc.tile_pool(name="two", bufs=2))
         ps_mm = ctx.enter_context(tc.psum_pool(name="ps_mm", bufs=4))
@@ -39,336 +36,371 @@ def tile_hopfield_euler_readout_t1_kernel(tc, x, w, a, d, c_bytes, c_scale, out)
         a_bf = keep.tile([P, 2, 4], BF16)
         d_bf = keep.tile([P, 2, 4], BF16)
         c_sc = keep.tile([P, 2, 4], F32)
-        nc.scalar.dma_start(out=a_bf[:], in_=a.rearrange("(g p t) -> p g t", p=P, t=4))
-        nc.scalar.dma_start(out=d_bf[:], in_=d.rearrange("(g p t) -> p g t", p=P, t=4))
-
         ident = keep.tile([P, P], F32)
-        make_identity(nc, ident[:])
-
-        x_tiles = {}
-
-        def load_x(i, hs=(0, 1)):
-            for h in hs:
-                x_sb = xin.tile([P, N], BF16, name="x_sb")
-                r0 = i * ROWS + h * P
-                nc.sync.dma_start(out=x_sb[:], in_=x[r0 : r0 + P, :])
-                x_tiles[(i, h)] = x_sb
-
+        c_by = keep.tile([P, 2, 4, R], U8, align_bytes=64)
+        a_f = keep.tile([P, 2, 4], F32)
+        d_f = keep.tile([P, 2, 4], F32)
+        warm = keep.tile([P, 1], F32)
+        warm2 = keep.tile([P, 1], F32)
         w_view = w.rearrange("(g p j) c -> g p j c", p=P, j=4)
-        w_raw = {}
+        x_sb, xt_ps, xg, xc, xs, t1, x1f, x1b, x1c, x1s, t2, x2b, x2c, x2s = ({} for _ in range(14))
+        w_raw, wc, ws, wg = {}, {}, {}, {}
+        cw, cg, cc, cs = {}, {}, {}, {}
+        s1, s2, y_ps = {}, {}, {}
+
+        def a_col(n):
+            return a_f[:, n // 4, n % 4 : n % 4 + 1]
+
+        def d_col(n):
+            return d_f[:, n // 4, n % 4 : n % 4 + 1]
+
+        def load_x(rt):
+            x_t = work.tile([P, N], BF16, name="x_t", bufs=8)
+            nc.sync.dma_start(out=x_t[:], in_=x[rt * P : rt * P + P, :])
+            x_sb[rt] = x_t
 
         def load_w(go, g):
             if g == 0:
-                w_sb = keep.tile([P, 2, 4, 512], BF16, name="w_raw%d" % go)
-                w_raw[go] = w_sb
-            if True:
-                nc.sync.dma_start(out=w_raw[go][:, g], in_=w_view[g][:, :, go * 512 : go * 512 + 512])
+                w_t = keep.tile([P, 2, 4, 512], BF16, name="w_raw%d" % go)
+                w_raw[go] = w_t
+            nc.sync.dma_start(out=w_raw[go][:, g], in_=w_view[g][:, :, go * 512 : go * 512 + 512])
 
-        c_by = keep.tile([P, 2, 4, R], U8, align_bytes=64)
+        def T(rt):
+            xt = ps_xt.tile([P, 2, 2, P], F32, name="xt")
+            words = x_sb[rt][:].bitcast(F32)
+            for g in range(2):
+                for u in range(2):
+                    nc.tensor.transpose(xt[:, g, u, :], words[:, 256 * g + u : 256 * g + 256 : 2], ident[:])
+            xt_ps[rt] = xt
 
-        with tc.manual_schedule():
-            warm = keep.tile([P, 1], F32)
-            nc.vector.memset(warm[:], 0.0)
-            warm2 = keep.tile([P, 1], F32)
-            nc.scalar.activation(warm2[:], warm[:], IDENT)
+        def XO(rt, eng="s"):
+            i, h = rt // 2, rt % 2
+            if rt % 4 == 0:
+                xg_t = two.tile([P, 2, 2, ROWS, 2], F32, name="xg_t", align_bytes=64)
+                xg[i // 2] = xg_t
+            o = xg[i // 2][:, i % 2, :, h * P : h * P + P, :]
+            i_ = xt_ps[rt][:].rearrange("p g u r -> p g r u")
+            if eng == "s":
+                nc.scalar.copy(out=o, in_=i_)
+            else:
+                nc.vector.tensor_copy(out=o, in_=i_)
 
-            load_x(0, (0,))
-            load_w(0, 0)
-            load_w(0, 1)
-            load_x(0, (1,))
-            load_w(1, 0)
-            load_w(1, 1)
-            load_x(1)
-            nc.sync.dma_start(out=c_by[:], in_=c_bytes.rearrange("(g p j) r -> p g j r", p=P, j=4))
-            nc.scalar.dma_start(out=c_sc[:], in_=c_scale.rearrange("(g p j) o -> p g (j o)", p=P, j=4))
-            load_x(2)
+        def QX(i):
+            xc_t = work.tile([P, 2, ROWS], U32, name="xc_t", align_bytes=64)
+            xs_t = work.tile([P, 2, ROWS], U8, name="xs_t", align_bytes=64)
+            xc[i], xs[i] = xc_t, xs_t
+            nc.vector.quantize_mx(
+                out=xc_t[:].rearrange("p g r -> p (g r)").bitcast(FP8X4),
+                scales=xs_t[:].rearrange("p g r -> p (g r)"),
+                in_=xg[i // 2][:, i % 2].rearrange("p g r u -> p (g r u)").bitcast(BF16),
+            )
 
-            a_f = keep.tile([P, 2, 4], F32)
-            d_f = keep.tile([P, 2, 4], F32)
-            nc.vector.tensor_copy(out=a_f[:], in_=a_bf[:])
-            nc.vector.tensor_copy(out=d_f[:], in_=d_bf[:])
+        t1_t = keep.tile([P, 8, ROWS], F32)
 
-            def a_col(n):
-                return a_f[:, n // 4, n % 4 : n % 4 + 1]
+        def TMP1(i, n, eng="g"):
+            q = i // 2
+            xv = xg[q][:].rearrange("p c g r u -> p (c g r u)").bitcast(BF16)
+            xv = xv.rearrange("p (c g r t) -> p c g r t", c=2, g=2, t=4)[:, i % 2, n // 4, :, n % 4]
+            o = t1_t[:, n, :]
+            if eng == "s":
+                nc.scalar.activation(o, xv, IDENT, bias=d_col(n), scale=a_col(n))
+            elif eng == "v":
+                nc.vector.tensor_scalar(out=o, in0=xv, scalar1=a_col(n), scalar2=d_col(n), op0=MULT, op1=ADD)
+            else:
+                nc.gpsimd.tensor_scalar(out=o, in0=xv, scalar1=a_col(n), scalar2=d_col(n), op0=MULT, op1=ADD)
 
-            def d_col(n):
-                return d_f[:, n // 4, n % 4 : n % 4 + 1]
-
-            xt_ps, xg, xc, xs, t1, x1f, x1b, x1c, x1s, t2, x2b, x2c, x2s = ({} for _ in range(13))
-            wc, ws, wg = {}, {}, {}
-            cw, cg, cc, cs = {}, {}, {}, {}
-            s1, s2, y_ps = {}, {}, {}
-
-            def T(i, hs=(0, 1)):
-                for h in hs:
-                    xt = ps_xt.tile([P, 2, 2, P], F32, name="xt")
-                    words = x_tiles[(i, h)][:].bitcast(F32)
-                    for g in range(2):
-                        for u in range(2):
-                            nc.tensor.transpose(xt[:, g, u, :], words[:, 256 * g + u : 256 * g + 256 : 2], ident[:])
-                    xt_ps[(i, h)] = xt
-
-            def XO(i, hs=(0, 1)):
-                if 0 in hs:
-                    xg_t = work.tile([P, 2, ROWS, 2], F32, name="xg_t", align_bytes=64)
-                    xg[i] = xg_t
-                for h in hs:
-                    nc.scalar.copy(
-                        out=xg[i][:, :, h * P : h * P + P, :], in_=xt_ps[(i, h)][:].rearrange("p g u r -> p g r u")
-                    )
-
-            def QX(i):
-                xc_t = work.tile([P, 2, ROWS], U32, name="xc_t", align_bytes=64)
-                xs_t = work.tile([P, 2, ROWS], U8, name="xs_t", align_bytes=64)
-                xc[i], xs[i] = xc_t, xs_t
-                nc.vector.quantize_mx(
-                    out=xc_t[:].rearrange("p g r -> p (g r)").bitcast(FP8X4),
-                    scales=xs_t[:].rearrange("p g r -> p (g r)"),
-                    in_=xg[i][:].rearrange("p g r u -> p (g r u)").bitcast(BF16),
-                )
-
-            def TMP1(i, gos=(0, 1)):
-                if 0 in gos:
-                    t1_t = two.tile([P, 8, ROWS], F32, name="t1_t")
-                    t1[i] = t1_t
-                xv = xg[i][:].rearrange("p g r u -> p (g r u)").bitcast(BF16).rearrange("p (g r t) -> p g r t", g=2, t=4)
-                for n in range(4 * gos[0], 4 * gos[-1] + 4):
-                    if i >= 2 and n == 7:
-                        nc.scalar.activation(t1[i][:, n, :], xv[:, n // 4, :, n % 4], IDENT, bias=d_col(n), scale=a_col(n))
-                    else:
-                        nc.vector.tensor_scalar(
-                            out=t1[i][:, n, :], in0=xv[:, n // 4, :, n % 4], scalar1=a_col(n), scalar2=d_col(n), op0=MULT, op1=ADD
-                        )
-
-            def S1(i, go):
-                for h in range(2):
-                    mm = ps_mm.tile([P, 2, ROWS], F32, name="mm")
-                    for tt in range(2):
-                        t = 2 * h + tt
-                        for g in range(2):
-                            nc.tensor.matmul_mx(
-                                out=mm[:, tt, :],
-                                lhsT=wc[go][:, g, t * P : t * P + P].bitcast(FP8X4),
-                                lhsT_scale=ws[go][:, g, t * P : t * P + P],
-                                rhs=xc[i][:, g, :].bitcast(FP8X4),
-                                rhs_scale=xs[i][:, g, :],
-                                start=(g == 0),
-                                stop=(g == 1),
-                            )
-                    s1[(i, go, h)] = mm
-
-            def A1(i, go):
-                if go == 0:
-                    x1f_t = two.tile([P, 8, ROWS], F32, name="x1f_t")
-                    x1f[i] = x1f_t
-                for h in range(2):
-                    n = 4 * go + 2 * h
-                    nc.vector.tensor_tensor(
-                        out=x1f[i][:, n : n + 2, :], in0=t1[i][:, n : n + 2, :], in1=s1[(i, go, h)][:], op=ADD
-                    )
-
-            def IL(i):
-                x1b_t = two.tile([P, 2, ROWS, 4], BF16, name="x1b_t", align_bytes=64)
-                x1b[i] = x1b_t
-                for go in range(2):
-                    nc.scalar.copy(
-                        out=x1b_t[:, go].rearrange("p (c i) t -> p c t i", i=4),
-                        in_=x1f[i][:, 4 * go : 4 * go + 4, :].rearrange("p t (c i) -> p c t i", i=4),
-                    )
-
-            def QX1(i):
-                x1c_t = two.tile([P, 2, ROWS], U32, name="x1c_t", align_bytes=64)
-                x1s_t = two.tile([P, 2, ROWS], U8, name="x1s_t", align_bytes=64)
-                x1c[i], x1s[i] = x1c_t, x1s_t
-                nc.vector.quantize_mx(
-                    out=x1c_t[:].rearrange("p g r -> p (g r)").bitcast(FP8X4),
-                    scales=x1s_t[:].rearrange("p g r -> p (g r)"),
-                    in_=x1b[i][:].rearrange("p g r t -> p (g r t)"),
-                )
-
-            def TMP2(i):
-                t2_t = two.tile([P, 8, ROWS], F32, name="t2_t")
-                t2[i] = t2_t
-                for n in range(8):
-                    if n in V2.get(i, ()):
-                        nc.vector.tensor_scalar(
-                            out=t2_t[:, n, :], in0=x1f[i][:, n, :], scalar1=a_col(n), scalar2=d_col(n), op0=MULT, op1=ADD
-                        )
-                    else:
-                        nc.scalar.activation(t2_t[:, n, :], x1f[i][:, n, :], IDENT, bias=d_col(n), scale=a_col(n))
-
-            def S2(i):
-                for h in range(2):
-                    for go in range(2):
-                        mm = ps_mm.tile([P, 4, P], F32, name="mm")
-                        for t in range(4):
-                            for g in range(2):
-                                nc.tensor.matmul_mx(
-                                    out=mm[:, t, :],
-                                    lhsT=wc[go][:, g, t * P : t * P + P].bitcast(FP8X4),
-                                    lhsT_scale=ws[go][:, g, t * P : t * P + P],
-                                    rhs=x1c[i][:, g, h * P : h * P + P].bitcast(FP8X4),
-                                    rhs_scale=x1s[i][:, g, h * P : h * P + P],
-                                    start=(g == 0),
-                                    stop=(g == 1),
-                                )
-                        s2[(i, go, h)] = mm
-
-            def A2(i, h):
-                if h == 0:
-                    x2b_t = two.tile([P, 2, 2, P, 4], BF16, name="x2b_t", align_bytes=64)
-                    x2b[i] = x2b_t
-                if True:
-                    for go in range(2):
-                        rs = slice(h * P, h * P + P)
-                        nc.vector.tensor_tensor(
-                            out=x2b[i][:, h, go].rearrange("p (c i) t -> p c t i", i=4),
-                            in0=t2[i][:, 4 * go : 4 * go + 4, rs].rearrange("p t (c i) -> p c t i", i=4),
-                            in1=s2[(i, go, h)][:].rearrange("p t (c i) -> p c t i", i=4),
-                            op=ADD,
-                        )
-
-            def QX2(i, h):
-                x2c_t = work.tile([P, 2, P], U32, name="x2c_t%d" % h, align_bytes=64)
-                x2s_t = work.tile([P, 2, P], U8, name="x2s_t%d" % h, align_bytes=64)
-                x2c[(i, h)], x2s[(i, h)] = x2c_t, x2s_t
-                nc.vector.quantize_mx(
-                    out=x2c_t[:].rearrange("p g r -> p (g r)").bitcast(FP8X4),
-                    scales=x2s_t[:].rearrange("p g r -> p (g r)"),
-                    in_=x2b[i][:, h].rearrange("p g r t -> p (g r t)"),
-                )
-
-            def S3(i):
-                for h in range(2):
-                    yp = ps_y.tile([P, R], F32, name="yp")
+        def S1(i, go):
+            for h in range(2):
+                mm = ps_mm.tile([P, 2, ROWS], F32, name="mm")
+                for tt in range(2):
+                    t = 2 * h + tt
                     for g in range(2):
                         nc.tensor.matmul_mx(
-                            out=yp[:],
-                            lhsT=x2c[(i, h)][:, g, :].bitcast(FP8X4),
-                            lhsT_scale=x2s[(i, h)][:, g, :],
-                            rhs=cc[0][:, g, :].bitcast(FP8X4),
-                            rhs_scale=cs[0][:, g, :],
+                            out=mm[:, tt, :],
+                            lhsT=wc[go][:, g, t * P : t * P + P].bitcast(FP8X4),
+                            lhsT_scale=ws[go][:, g, t * P : t * P + P],
+                            rhs=xc[i][:, g, :].bitcast(FP8X4),
+                            rhs_scale=xs[i][:, g, :],
                             start=(g == 0),
                             stop=(g == 1),
                         )
-                    y_ps[(i, h)] = yp
+                s1[(i, go, h)] = mm
 
-            def YO(i):
-                for h in range(2):
-                    y_sb = work.tile([P, R], F32, name="y_sb", bufs=6)
-                    nc.scalar.copy(out=y_sb[:], in_=y_ps[(i, h)][:])
-                    r0 = i * ROWS + h * P
-                    nc.sync.dma_start(out=out[r0 : r0 + P, :], in_=y_sb[:])
+        def A1(i, k):
+            if k == 0:
+                x1f_t = two.tile([P, 8, ROWS], F32, name="x1f_t")
+                x1f[i] = x1f_t
+            nc.vector.tensor_tensor(
+                out=x1f[i][:, 2 * k : 2 * k + 2, :],
+                in0=t1_t[:, 2 * k : 2 * k + 2, :],
+                in1=s1[(i, k // 2, k % 2)][:],
+                op=ADD,
+            )
 
-            def WI(go, g, eng, t0=0, t1_=4):
-                if go not in wg:
-                    wg_t = keep.tile([P, 2, 512, 4], BF16, name="wg%d" % go, align_bytes=64)
-                    wg[go] = wg_t
-                o = wg[go][:, g].rearrange("p (t m) j -> p t m j", t=4)[:, t0:t1_]
-                i_ = w_raw[go][:, g].rearrange("p j (m t) -> p t m j", t=4)[:, t0:t1_]
-                if eng == "v":
-                    nc.vector.tensor_copy(out=o, in_=i_)
-                else:
-                    nc.scalar.copy(out=o, in_=i_)
+        def IL(i, go, eng="s"):
+            if go == 0:
+                x1b_t = two.tile([P, 2, ROWS, 4], BF16, name="x1b_t", align_bytes=64)
+                x1b[i] = x1b_t
+            nc.scalar.copy(
+                out=x1b[i][:, go].rearrange("p (c i) t -> p c t i", i=4),
+                in_=x1f[i][:, 4 * go : 4 * go + 4, :].rearrange("p t (c i) -> p c t i", i=4),
+            )
 
-            def WQ(go):
-                wc_t = keep.tile([P, 2, 512], U32, name="wc%d" % go, align_bytes=64)
-                ws_t = keep.tile([P, 2, 512], U8, name="ws%d" % go, align_bytes=64)
-                wc[go], ws[go] = wc_t, ws_t
-                nc.vector.quantize_mx(
-                    out=wc_t[:].rearrange("p g c -> p (g c)").bitcast(FP8X4),
-                    scales=ws_t[:].rearrange("p g c -> p (g c)"),
-                    in_=wg[go][:].rearrange("p g c j -> p (g c j)"),
+        def QX1(i):
+            x1c_t = two.tile([P, 2, ROWS], U32, name="x1c_t", align_bytes=64)
+            x1s_t = two.tile([P, 2, ROWS], U8, name="x1s_t", align_bytes=64)
+            x1c[i], x1s[i] = x1c_t, x1s_t
+            nc.vector.quantize_mx(
+                out=x1c_t[:].rearrange("p g r -> p (g r)").bitcast(FP8X4),
+                scales=x1s_t[:].rearrange("p g r -> p (g r)"),
+                in_=x1b[i][:].rearrange("p g r t -> p (g r t)"),
+            )
+
+        def TMP2(i, n):
+            if n == 0:
+                t2_t = two.tile([P, 8, ROWS], F32, name="t2_t")
+                t2[i] = t2_t
+            if n in V2.get(i, ()):
+                nc.vector.tensor_scalar(
+                    out=t2[i][:, n, :], in0=x1f[i][:, n, :], scalar1=a_col(n), scalar2=d_col(n), op0=MULT, op1=ADD
                 )
+            else:
+                nc.scalar.activation(t2[i][:, n, :], x1f[i][:, n, :], IDENT, bias=d_col(n), scale=a_col(n))
 
-            def CW(g):
+        def S2(i):
+            for h in range(2):
+                for go in range(2):
+                    mm = ps_mm.tile([P, 4, P], F32, name="mm")
+                    for t in range(4):
+                        for g in range(2):
+                            nc.tensor.matmul_mx(
+                                out=mm[:, t, :],
+                                lhsT=wc[go][:, g, t * P : t * P + P].bitcast(FP8X4),
+                                lhsT_scale=ws[go][:, g, t * P : t * P + P],
+                                rhs=x1c[i][:, g, h * P : h * P + P].bitcast(FP8X4),
+                                rhs_scale=x1s[i][:, g, h * P : h * P + P],
+                                start=(g == 0),
+                                stop=(g == 1),
+                            )
+                    s2[(i, go, h)] = mm
+
+        def A2(i, k):
+            h, go = k // 2, k % 2
+            if k == 0:
+                x2b_t = two.tile([P, 2, 2, P, 4], BF16, name="x2b_t", align_bytes=64)
+                x2b[i] = x2b_t
+            rs = slice(h * P, h * P + P)
+            nc.vector.tensor_tensor(
+                out=x2b[i][:, h, go].rearrange("p (c i) t -> p c t i", i=4),
+                in0=t2[i][:, 4 * go : 4 * go + 4, rs].rearrange("p t (c i) -> p c t i", i=4),
+                in1=s2[(i, go, h)][:].rearrange("p t (c i) -> p c t i", i=4),
+                op=ADD,
+            )
+
+        def QX2(i, h0, h1):
+            if h0 == 0:
+                x2c_t = work.tile([P, 2, 2, P], U32, name="x2c_t", bufs=4, align_bytes=64)
+                x2s_t = work.tile([P, 2, 2, P], U8, name="x2s_t", bufs=4, align_bytes=64)
+                x2c[i], x2s[i] = x2c_t, x2s_t
+            nc.vector.quantize_mx(
+                out=x2c[i][:, h0:h1].rearrange("p h g r -> p (h g r)").bitcast(FP8X4),
+                scales=x2s[i][:, h0:h1].rearrange("p h g r -> p (h g r)"),
+                in_=x2b[i][:, h0:h1].rearrange("p h g r t -> p (h g r t)"),
+            )
+
+        def S3(i, h, parts=1):
+            wd = R // parts
+            for q in range(parts):
+                yp = ps_y.tile([P, wd], F32, name="yp")
+                for g in range(2):
+                    nc.tensor.matmul_mx(
+                        out=yp[:],
+                        lhsT=x2c[i][:, h, g, :].bitcast(FP8X4),
+                        lhsT_scale=x2s[i][:, h, g, :],
+                        rhs=cc[0][:, g, q * wd : q * wd + wd].bitcast(FP8X4),
+                        rhs_scale=cs[0][:, g, q * wd : q * wd + wd],
+                        start=(g == 0),
+                        stop=(g == 1),
+                    )
+                y_ps[(i, h, q)] = yp
+
+        def YO(i, h, parts=1):
+            wd = R // parts
+            for q in range(parts):
+                y_sb = work.tile([P, wd], F32, name="y_sb" if parts == 1 else "y_half", bufs=6 if parts == 1 else 2)
+                if q == 0:
+                    nc.scalar.copy(out=y_sb[:], in_=y_ps[(i, h, q)][:])
+                else:
+                    nc.vector.tensor_copy(out=y_sb[:], in_=y_ps[(i, h, q)][:])
+                r0 = i * ROWS + h * P
+                eng = nc.sync if q == 0 else nc.scalar
+                eng.dma_start(out=out[r0 : r0 + P, q * wd : q * wd + wd], in_=y_sb[:])
+
+        def WI(go, g, eng, t0=0, t1_=4):
+            if go not in wg:
+                wg_t = keep.tile([P, 2, 512, 4], BF16, name="wg%d" % go, align_bytes=64)
+                wg[go] = wg_t
+            o = wg[go][:, g].rearrange("p (t m) j -> p t m j", t=4)[:, t0:t1_]
+            i_ = w_raw[go][:, g].rearrange("p j (m t) -> p t m j", t=4)[:, t0:t1_]
+            if eng == "v":
+                nc.vector.tensor_copy(out=o, in_=i_)
+            else:
+                nc.scalar.copy(out=o, in_=i_)
+
+        def WQ(go):
+            wc_t = keep.tile([P, 2, 512], U32, name="wc%d" % go, align_bytes=64)
+            ws_t = keep.tile([P, 2, 512], U8, name="ws%d" % go, align_bytes=64)
+            wc[go], ws[go] = wc_t, ws_t
+            nc.vector.quantize_mx(
+                out=wc_t[:].rearrange("p g c -> p (g c)").bitcast(FP8X4),
+                scales=ws_t[:].rearrange("p g c -> p (g c)"),
+                in_=wg[go][:].rearrange("p g c j -> p (g c j)"),
+            )
+
+        def CW(g, j, eng):
+            if g not in cw:
                 cw_t = keep.tile([P, 4, R], BF16, name="cw%d" % g)
                 cw[g] = cw_t
-                for j in range(4):
-                    nc.vector.tensor_scalar(
-                        out=cw_t[:, j, :], in0=c_by[:, g, j, :].bitcast(FP8), scalar1=c_sc[:, g, j : j + 1], scalar2=None, op0=MULT
-                    )
+            i_ = c_by[:, g, j, :].bitcast(FP8)
+            if eng == "v":
+                nc.vector.tensor_scalar(out=cw[g][:, j, :], in0=i_, scalar1=c_sc[:, g, j : j + 1], scalar2=None, op0=MULT)
+            else:
+                nc.scalar.activation(cw[g][:, j, :], i_, mybir.ActivationFunctionType.Copy, scale=c_sc[:, g, j : j + 1])
 
-            def CI(g):
-                if 0 not in cg:
-                    cg_t = keep.tile([P, 2, R, 4], BF16, name="cg", align_bytes=64)
-                    cg[0] = cg_t
-                nc.scalar.copy(out=cg[0][:, g], in_=cw[g][:].rearrange("p j r -> p r j"))
+        def CI(g, eng="s"):
+            if 0 not in cg:
+                cg_t = keep.tile([P, 2, R, 4], BF16, name="cg", align_bytes=64)
+                cg[0] = cg_t
+            o = cg[0][:, g].rearrange("p (c i) j -> p c j i", i=4)
+            i_ = cw[g][:].rearrange("p j (c i) -> p c j i", i=4)
+            if eng == "s":
+                nc.scalar.copy(out=o, in_=i_)
+            else:
+                nc.vector.tensor_copy(out=o, in_=i_)
 
-            def CQ():
-                cc_t = keep.tile([P, 2, R], U32, name="cc", align_bytes=64)
-                cs_t = keep.tile([P, 2, R], U8, name="cs", align_bytes=64)
-                cc[0], cs[0] = cc_t, cs_t
-                nc.vector.quantize_mx(
-                    out=cc_t[:].rearrange("p g r -> p (g r)").bitcast(FP8X4),
-                    scales=cs_t[:].rearrange("p g r -> p (g r)"),
-                    in_=cg[0][:].rearrange("p g r j -> p (g r j)"),
-                )
+        def CQ():
+            cc_t = keep.tile([P, 2, R], U32, name="cc", align_bytes=64)
+            cs_t = keep.tile([P, 2, R], U8, name="cs", align_bytes=64)
+            cc[0], cs[0] = cc_t, cs_t
+            nc.vector.quantize_mx(
+                out=cc_t[:].rearrange("p g r -> p (g r)").bitcast(FP8X4),
+                scales=cs_t[:].rearrange("p g r -> p (g r)"),
+                in_=cg[0][:].rearrange("p g r j -> p (g r j)"),
+            )
 
-            T(0, (0,))
-            XO(0, (0,))
+        with tc.manual_schedule():
+            nc.scalar.dma_start(out=a_bf[:], in_=a.rearrange("(g p t) -> p g t", p=P, t=4))
+            nc.scalar.dma_start(out=d_bf[:], in_=d.rearrange("(g p t) -> p g t", p=P, t=4))
+            nc.vector.memset(warm[:], 0.0)
+            nc.scalar.activation(warm2[:], warm[:], IDENT)
+            make_identity(nc, ident[:])
+            load_x(0)
+            load_w(0, 0)
+            load_w(0, 1)
+            load_x(1)
+            load_w(1, 0)
+            load_w(1, 1)
+            load_x(2)
+            load_x(3)
+            nc.sync.dma_start(out=c_by[:], in_=c_bytes.rearrange("(g p j) r -> p g j r", p=P, j=4))
+            nc.scalar.dma_start(out=c_sc[:], in_=c_scale.rearrange("(g p j) o -> p g (j o)", p=P, j=4))
+            for rt in range(4, 8):
+                load_x(rt)
+            nc.gpsimd.tensor_copy(out=a_f[:], in_=a_bf[:])
+            nc.gpsimd.tensor_copy(out=d_f[:], in_=d_bf[:])
+
+            T(0)
+            XO(0)
             WI(0, 0, "v")
             WI(0, 1, "s", 2, 4)
             WI(0, 1, "v", 0, 2)
-            T(0, (1,))
-            XO(0, (1,))
-            WQ(0)
-            QX(0)
-            TMP1(0)
-            WI(1, 0, "v", 0, 2)
-            WI(1, 0, "s", 2, 4)
-            WI(1, 1, "s")
-            S1(0, 0)
-            A1(0, 0)
             T(1)
             XO(1)
+            WQ(0)
+            QX(0)
+            S1(0, 0)
+            WI(1, 0, "v", 0, 2)
+            WI(1, 0, "s", 2, 4)
+            for n in range(4):
+                TMP1(0, n, "v")
+            for n in range(4, 8):
+                TMP1(0, n, "g")
+            WI(1, 1, "v", 0, 2)
+            WI(1, 1, "s", 2, 4)
             WQ(1)
-            S1(0, 1)
-            QX(1)
-            A1(0, 1)
-            IL(0)
-            TMP1(1)
             T(2)
+            T(3)
+            S1(0, 1)
             XO(2)
+            XO(3)
+            A1(0, 0)
+            A1(0, 1)
+            QX(1)
+            for n in range(4):
+                TMP1(1, n, "g")
+            A1(0, 2)
+            A1(0, 3)
+            IL(0, 0)
+            IL(0, 1)
+            for n in range(4, 8):
+                TMP1(1, n)
+            for g in (0,):
+                for j in range(4):
+                    CW(g, j, "v")
+            for rt in range(4, 6):
+                T(rt)
+                XO(rt)
             QX1(0)
+
             for i in range(CHUNKS + 1):
-                if i + 3 < CHUNKS:
-                    load_x(i + 3)
+                if i < 2:
+                    for rt in (2 * i + 8, 2 * i + 9):
+                        load_x(rt)
                 if i + 1 < CHUNKS:
                     S1(i + 1, 0)
                     S1(i + 1, 1)
                 if i < CHUNKS:
-                    TMP2(i)
-                if i + 1 < CHUNKS:
-                    A1(i + 1, 0)
-                    A1(i + 1, 1)
+                    for n in range(8):
+                        TMP2(i, n)
+                for k in range(4):
+                    if i + 1 < CHUNKS:
+                        A1(i + 1, k)
+                        if i + 2 < CHUNKS:
+                            TMP1(i + 2, 2 * k)
+                            TMP1(i + 2, 2 * k + 1)
                 if i < CHUNKS:
                     S2(i)
-                if i == 2:
-                    CQ()
-                    S3(0)
-                if i >= 2:
-                    S3(i - 1)
                 if i + 1 < CHUNKS:
-                    IL(i + 1)
+                    IL(i + 1, 0)
+                    IL(i + 1, 1)
+                if i == 3:
+                    CQ()
+                if i >= 3:
+                    for j in {3: (0, 1), 4: (2, 3), 5: (4,), 6: (5,)}[i]:
+                        last = j == CHUNKS - 1
+                        for h in range(2):
+                            S3(j, h, 2 if last and h else 1)
+                            YO(j, h, 2 if last and h else 1)
+                if i < 3:
+                    for rt in (2 * i + 6, 2 * i + 7):
+                        T(rt)
+                        XO(rt)
+                for k in range(4):
+                    if i < CHUNKS:
+                        A2(i, k)
+                        if k == 1 and i + 2 < CHUNKS:
+                            QX(i + 2)
+                        if i == CHUNKS - 1 and k == 2:
+                            QX2(i, 0, 1)
                 if i == 2:
-                    YO(0)
-                if i >= 2:
-                    YO(i - 1)
-                if i + 2 < CHUNKS:
-                    QX(i + 2)
-                    TMP1(i + 2)
-                if i + 3 < CHUNKS:
-                    T(i + 3)
-                    XO(i + 3)
-                if i < 2:
-                    CW(i)
-                    CI(i)
-                if i < CHUNKS:
-                    A2(i, 0)
-                    A2(i, 1)
+                    for j in range(4):
+                        CW(1, j, "v")
+                if i == 2:
+                    CI(0)
+                    CI(1)
                 if i + 1 < CHUNKS:
                     QX1(i + 1)
-                if i < CHUNKS:
-                    QX2(i, 0)
-                    QX2(i, 1)
+                if i < CHUNKS - 1:
+                    QX2(i, 0, 2)
+                if i == CHUNKS - 1:
+                    QX2(i, 1, 2)

@@ -7,8 +7,11 @@ M, N, R = 1536, 1024, 512
 FLOPS = 2 * M * N * (N + N + R)
 
 P = 128
+SLOTS = 4
+HALF = P * SLOTS
 ROWS = 256
 CHUNKS = M // ROWS
+LAST = CHUNKS - 1
 
 F32 = mybir.dt.float32
 BF16 = mybir.dt.bfloat16
@@ -18,282 +21,287 @@ FP8 = mybir.dt.float8_e4m3fn
 FP8X4 = mybir.dt.float8_e4m3fn_x4
 ADD = mybir.AluOpType.add
 MULT = mybir.AluOpType.mult
-IDENT = mybir.ActivationFunctionType.Identity
-V2 = {5: (1, 3, 5, 7)}
-S1N = ()
+COPY = mybir.ActivationFunctionType.Copy
+IDENTITY = mybir.ActivationFunctionType.Identity
+
+READOUT_STEPS = {3: (0, 1, 2), 4: (3,), 5: (4,), 6: (5,)}
+
+
+def blocks_of_four(interleaved, by_slot):
+    return (
+        interleaved.rearrange("p (c i) t -> p c t i", i=4),
+        by_slot.rearrange("p t (c i) -> p c t i", i=4),
+    )
 
 
 def tile_hopfield_euler_readout_t1_kernel(tc, x, w, a, d, c_bytes, c_scale, out):
     nc = tc.nc
+
     with ExitStack() as ctx:
         keep = ctx.enter_context(tc.tile_pool(name="keep", bufs=1))
-        work = ctx.enter_context(tc.tile_pool(name="work", bufs=3))
-        two = ctx.enter_context(tc.tile_pool(name="two", bufs=2))
-        ps_mm = ctx.enter_context(tc.psum_pool(name="ps_mm", bufs=4))
-        ps_xt = ctx.enter_context(tc.psum_pool(name="ps_xt", bufs=2))
-        ps_y = ctx.enter_context(tc.psum_pool(name="ps_y", bufs=2))
+        stream = ctx.enter_context(tc.tile_pool(name="stream", bufs=2))
+        x_pool = ctx.enter_context(tc.tile_pool(name="x_pool", bufs=3))
+        x2_pool = ctx.enter_context(tc.tile_pool(name="x2_pool", bufs=4))
+        y_pool = ctx.enter_context(tc.tile_pool(name="y_pool", bufs=4))
+        psum_step = ctx.enter_context(tc.psum_pool(name="psum_step", bufs=4))
+        psum_turn = ctx.enter_context(tc.psum_pool(name="psum_turn", bufs=2))
+        psum_y = ctx.enter_context(tc.psum_pool(name="psum_y", bufs=2))
 
-        a_bf = keep.tile([P, 2, 4], BF16)
-        d_bf = keep.tile([P, 2, 4], BF16)
-        c_sc = keep.tile([P, 2, 4], F32)
-        ident = keep.tile([P, P], F32)
-        c_by = keep.tile([P, 2, 4, R], U8, align_bytes=64)
-        a_f = keep.tile([P, 2, 4], F32)
-        d_f = keep.tile([P, 2, 4], F32)
-        warm = keep.tile([P, 1], F32)
-        warm2 = keep.tile([P, 1], F32)
-        w_view = w.rearrange("(g p j) c -> g p j c", p=P, j=4)
-        x_sb, xt_ps, xg, xc, xs, t1, x1f, x1b, x1c, x1s, t2, x2b, x2c, x2s = ({} for _ in range(14))
-        w_raw, wc, ws, wg = {}, {}, {}, {}
-        cw, cg, cc, cs = {}, {}, {}, {}
-        s1, s2, y_ps = {}, {}, {}
+        identity = keep.tile([P, P], F32)
+        a_bf16 = keep.tile([P, 2, SLOTS], BF16)
+        d_bf16 = keep.tile([P, 2, SLOTS], BF16)
+        a_f32 = keep.tile([P, 2, SLOTS], F32)
+        d_f32 = keep.tile([P, 2, SLOTS], F32)
+        c_scales_in = keep.tile([P, 2, SLOTS], F32)
+        c_bytes_in = keep.tile([P, 2, SLOTS, R], U8, align_bytes=64)
+        c_wide = keep.tile([P, 2, SLOTS, R], BF16)
+        c_mixed = keep.tile([P, 2, R, SLOTS], BF16, align_bytes=64)
+        c_codes = keep.tile([P, 2, R], U32, align_bytes=64)
+        c_scales = keep.tile([P, 2, R], U8, align_bytes=64)
+        table_in = keep.tile([P, 1], F32)
+        table_out = keep.tile([P, 1], F32)
+        w_in, w_mixed, w_codes, w_scales = [], [], [], []
+        for h in range(2):
+            w_in.append(keep.tile([P, 2, SLOTS, HALF], BF16, name="w_in%d" % h))
+            w_mixed.append(keep.tile([P, 2, HALF, SLOTS], BF16, name="w_mixed%d" % h, align_bytes=64))
+            w_codes.append(keep.tile([P, 2, HALF], U32, name="w_codes%d" % h, align_bytes=64))
+            w_scales.append(keep.tile([P, 2, HALF], U8, name="w_scales%d" % h, align_bytes=64))
+        x_in = [keep.tile([P, N], BF16, name="x_in%d" % r) for r in range(M // P)]
 
-        def a_col(n):
-            return a_f[:, n // 4, n % 4 : n % 4 + 1]
+        x_mixed, leak1, x1, x1_mixed, leak2, x2_mixed = {}, {}, {}, {}, {}, {}
+        x_q, x1_q, x2_q = {}, {}, {}
+        turned, product1, product2, y_banks = {}, {}, {}, {}
 
-        def d_col(n):
-            return d_f[:, n // 4, n % 4 : n % 4 + 1]
+        def column(tile, n):
+            return tile[:, n // SLOTS, n % SLOTS : n % SLOTS + 1]
 
-        def load_x(rt):
-            x_t = work.tile([P, N], BF16, name="x_t", bufs=8)
-            nc.sync.dma_start(out=x_t[:], in_=x[rt * P : rt * P + P, :])
-            x_sb[rt] = x_t
+        def quantize(out_codes, out_scales, values):
+            nc.vector.quantize_mx(out=out_codes.bitcast(FP8X4), scales=out_scales, in_=values)
 
-        def load_w(go, g):
-            if g == 0:
-                w_t = keep.tile([P, 2, 4, 512], BF16, name="w_raw%d" % go)
-                w_raw[go] = w_t
-            nc.sync.dma_start(out=w_raw[go][:, g], in_=w_view[g][:, :, go * 512 : go * 512 + 512])
+        def multiply(bank, stationary, stationary_cols, moving, moving_cols):
+            for g in range(2):
+                nc.tensor.matmul_mx(
+                    out=bank,
+                    lhsT=stationary[0][:, g, stationary_cols].bitcast(FP8X4),
+                    lhsT_scale=stationary[1][:, g, stationary_cols],
+                    rhs=moving[0][:, g, moving_cols].bitcast(FP8X4),
+                    rhs_scale=moving[1][:, g, moving_cols],
+                    start=(g == 0),
+                    stop=(g == 1),
+                )
 
-        def T(rt):
-            xt = ps_xt.tile([P, 2, 2, P], F32, name="xt")
-            words = x_sb[rt][:].bitcast(F32)
+
+        def load_w(h, g):
+            rows = w[g * HALF : (g + 1) * HALF, h * HALF : (h + 1) * HALF]
+            nc.sync.dma_start(out=w_in[h][:, g], in_=rows.rearrange("(p j) c -> p j c", j=SLOTS))
+
+        def interleave_w(copy, h, g, slots):
+            copy(
+                out=w_mixed[h][:, g].rearrange("p (t m) j -> p t m j", t=SLOTS)[:, slots],
+                in_=w_in[h][:, g].rearrange("p j (m t) -> p t m j", t=SLOTS)[:, slots],
+            )
+
+        def share_interleave_w(h, g):
+            interleave_w(nc.vector.tensor_copy, h, g, slice(0, 2))
+            interleave_w(nc.scalar.copy, h, g, slice(2, 4))
+
+        def quantize_w(h):
+            quantize(
+                w_codes[h][:].rearrange("p g c -> p (g c)"),
+                w_scales[h][:].rearrange("p g c -> p (g c)"),
+                w_mixed[h][:].rearrange("p g c j -> p (g c j)"),
+            )
+
+
+        def load_c(g):
+            rows = c_bytes[g * HALF : (g + 1) * HALF, :]
+            nc.sync.dma_start(out=c_bytes_in[:, g], in_=rows.rearrange("(p j) r -> p j r", j=SLOTS))
+
+        def widen_c(g):
+            for j in range(SLOTS):
+                values, scale = c_bytes_in[:, g, j, :].bitcast(FP8), c_scales_in[:, g, j : j + 1]
+                if g == 0 and j < 2:
+                    nc.scalar.activation(c_wide[:, g, j, :], values, COPY, scale=scale)
+                else:
+                    nc.vector.tensor_scalar(out=c_wide[:, g, j, :], in0=values, scalar1=scale, scalar2=None, op0=MULT)
+
+        def interleave_c(g):
+            mixed, by_slot = blocks_of_four(c_mixed[:, g], c_wide[:, g])
+            nc.scalar.copy(out=mixed, in_=by_slot)
+
+        def quantize_c():
+            quantize(
+                c_codes[:].rearrange("p g r -> p (g r)"),
+                c_scales[:].rearrange("p g r -> p (g r)"),
+                c_mixed[:].rearrange("p g r j -> p (g r j)"),
+            )
+
+
+        def load_x(r):
+            nc.sync.dma_start(out=x_in[r][:], in_=x[r * P : (r + 1) * P, :])
+
+        def turn_x(r):
+            bank = psum_turn.tile([P, 2, 2, P], F32, name="bank_turned")
+            words = x_in[r][:].bitcast(F32)
             for g in range(2):
                 for u in range(2):
-                    nc.tensor.transpose(xt[:, g, u, :], words[:, 256 * g + u : 256 * g + 256 : 2], ident[:])
-            xt_ps[rt] = xt
+                    nc.tensor.transpose(bank[:, g, u, :], words[:, 256 * g + u : 256 * (g + 1) : 2], identity[:])
+            turned[r] = bank
 
-        def XO(rt, eng="s"):
-            i, h = rt // 2, rt % 2
-            if rt % 4 == 0:
-                xg_t = two.tile([P, 2, 2, ROWS, 2], F32, name="xg_t", align_bytes=64)
-                xg[i // 2] = xg_t
-            o = xg[i // 2][:, i % 2, :, h * P : h * P + P, :]
-            i_ = xt_ps[rt][:].rearrange("p g u r -> p g r u")
-            if eng == "s":
-                nc.scalar.copy(out=o, in_=i_)
-            else:
-                nc.vector.tensor_copy(out=o, in_=i_)
-
-        def QX(i):
-            xc_t = work.tile([P, 2, ROWS], U32, name="xc_t", align_bytes=64)
-            xs_t = work.tile([P, 2, ROWS], U8, name="xs_t", align_bytes=64)
-            xc[i], xs[i] = xc_t, xs_t
-            nc.vector.quantize_mx(
-                out=xc_t[:].rearrange("p g r -> p (g r)").bitcast(FP8X4),
-                scales=xs_t[:].rearrange("p g r -> p (g r)"),
-                in_=xg[i // 2][:, i % 2].rearrange("p g r u -> p (g r u)").bitcast(BF16),
-            )
-
-        t1_t = keep.tile([P, 8, ROWS], F32)
-
-        def TMP1(i, n, eng="g"):
-            q = i // 2
-            xv = xg[q][:].rearrange("p c g r u -> p (c g r u)").bitcast(BF16)
-            xv = xv.rearrange("p (c g r t) -> p c g r t", c=2, g=2, t=4)[:, i % 2, n // 4, :, n % 4]
-            o = t1_t[:, n, :]
-            if eng == "s":
-                nc.scalar.activation(o, xv, IDENT, bias=d_col(n), scale=a_col(n))
-            elif eng == "v":
-                nc.vector.tensor_scalar(out=o, in0=xv, scalar1=a_col(n), scalar2=d_col(n), op0=MULT, op1=ADD)
-            else:
-                nc.gpsimd.tensor_scalar(out=o, in0=xv, scalar1=a_col(n), scalar2=d_col(n), op0=MULT, op1=ADD)
-
-        def S1(i, go):
-            for h in range(2):
-                mm = ps_mm.tile([P, 2, ROWS], F32, name="mm")
-                for tt in range(2):
-                    t = 2 * h + tt
-                    for g in range(2):
-                        nc.tensor.matmul_mx(
-                            out=mm[:, tt, :],
-                            lhsT=wc[go][:, g, t * P : t * P + P].bitcast(FP8X4),
-                            lhsT_scale=ws[go][:, g, t * P : t * P + P],
-                            rhs=xc[i][:, g, :].bitcast(FP8X4),
-                            rhs_scale=xs[i][:, g, :],
-                            start=(g == 0),
-                            stop=(g == 1),
-                        )
-                s1[(i, go, h)] = mm
-
-        def A1(i, k):
-            if k == 0:
-                x1f_t = two.tile([P, 8, ROWS], F32, name="x1f_t")
-                x1f[i] = x1f_t
-            nc.vector.tensor_tensor(
-                out=x1f[i][:, 2 * k : 2 * k + 2, :],
-                in0=t1_t[:, 2 * k : 2 * k + 2, :],
-                in1=s1[(i, k // 2, k % 2)][:],
-                op=ADD,
-            )
-
-        def IL(i, go, eng="s"):
-            if go == 0:
-                x1b_t = two.tile([P, 2, ROWS, 4], BF16, name="x1b_t", align_bytes=64)
-                x1b[i] = x1b_t
+        def copy_turned(r):
+            chunk, r0 = r // 2, (r % 2) * P
+            if r % 4 == 0:
+                x_mixed_pair = stream.tile([P, 2, 2, ROWS, 2], F32, name="x_mixed_pair", align_bytes=64)
+                x_mixed[chunk // 2] = x_mixed_pair
             nc.scalar.copy(
-                out=x1b[i][:, go].rearrange("p (c i) t -> p c t i", i=4),
-                in_=x1f[i][:, 4 * go : 4 * go + 4, :].rearrange("p t (c i) -> p c t i", i=4),
+                out=x_mixed[chunk // 2][:, chunk % 2, :, r0 : r0 + P, :],
+                in_=turned[r][:].rearrange("p g u r -> p g r u"),
             )
 
-        def QX1(i):
-            x1c_t = two.tile([P, 2, ROWS], U32, name="x1c_t", align_bytes=64)
-            x1s_t = two.tile([P, 2, ROWS], U8, name="x1s_t", align_bytes=64)
-            x1c[i], x1s[i] = x1c_t, x1s_t
-            nc.vector.quantize_mx(
-                out=x1c_t[:].rearrange("p g r -> p (g r)").bitcast(FP8X4),
-                scales=x1s_t[:].rearrange("p g r -> p (g r)"),
-                in_=x1b[i][:].rearrange("p g r t -> p (g r t)"),
+        def quantize_x(i):
+            x_codes = x_pool.tile([P, 2, ROWS], U32, name="x_codes", align_bytes=64)
+            x_scales = x_pool.tile([P, 2, ROWS], U8, name="x_scales", align_bytes=64)
+            x_q[i] = (x_codes, x_scales)
+            quantize(
+                x_codes[:].rearrange("p g r -> p (g r)"),
+                x_scales[:].rearrange("p g r -> p (g r)"),
+                x_mixed[i // 2][:, i % 2].rearrange("p g r u -> p (g r u)").bitcast(BF16),
             )
 
-        def TMP2(i, n):
-            if n == 0:
-                t2_t = two.tile([P, 8, ROWS], F32, name="t2_t")
-                t2[i] = t2_t
-            if n in V2.get(i, ()):
+
+        def leak_x(on_scalar, pair, n, first=0, count=2):
+            if pair not in leak1:
+                leak1_pair = stream.tile([P, 2, 2 * SLOTS, ROWS], F32, name="leak1_pair")
+                leak1[pair] = leak1_pair
+            chunks = slice(first, first + count)
+            values = x_mixed[pair][:].rearrange("p c g r u -> p (c g r u)").bitcast(BF16)
+            values = values.rearrange("p (c g r t) -> p c g r t", c=2, g=2, t=SLOTS)
+            values = values[:, chunks, n // SLOTS, :, n % SLOTS]
+            leak = leak1[pair][:, chunks, n, :]
+            if on_scalar:
+                nc.scalar.activation(leak, values, IDENTITY, bias=column(d_f32, n), scale=column(a_f32, n))
+            else:
                 nc.vector.tensor_scalar(
-                    out=t2[i][:, n, :], in0=x1f[i][:, n, :], scalar1=a_col(n), scalar2=d_col(n), op0=MULT, op1=ADD
+                    out=leak, in0=values, scalar1=column(a_f32, n), scalar2=column(d_f32, n), op0=MULT, op1=ADD
                 )
-            else:
-                nc.scalar.activation(t2[i][:, n, :], x1f[i][:, n, :], IDENT, bias=d_col(n), scale=a_col(n))
 
-        def S2(i):
-            for h in range(2):
-                for go in range(2):
-                    mm = ps_mm.tile([P, 4, P], F32, name="mm")
-                    for t in range(4):
-                        for g in range(2):
-                            nc.tensor.matmul_mx(
-                                out=mm[:, t, :],
-                                lhsT=wc[go][:, g, t * P : t * P + P].bitcast(FP8X4),
-                                lhsT_scale=ws[go][:, g, t * P : t * P + P],
-                                rhs=x1c[i][:, g, h * P : h * P + P].bitcast(FP8X4),
-                                rhs_scale=x1s[i][:, g, h * P : h * P + P],
-                                start=(g == 0),
-                                stop=(g == 1),
-                            )
-                    s2[(i, go, h)] = mm
+        def multiply1(i, h):
+            for b in range(2):
+                bank = psum_step.tile([P, 2, ROWS], F32, name="bank_step")
+                for s in range(2):
+                    t = 2 * b + s
+                    multiply(bank[:, s, :], (w_codes[h], w_scales[h]), slice(t * P, (t + 1) * P), x_q[i], slice(0, ROWS))
+                product1[(i, 2 * h + b)] = bank
 
-        def A2(i, k):
-            h, go = k // 2, k % 2
-            if k == 0:
-                x2b_t = two.tile([P, 2, 2, P, 4], BF16, name="x2b_t", align_bytes=64)
-                x2b[i] = x2b_t
-            rs = slice(h * P, h * P + P)
+        def add1(i, b):
+            if b == 0:
+                x1_chunk = stream.tile([P, 2 * SLOTS, ROWS], F32, name="x1_chunk")
+                x1[i] = x1_chunk
+            two_slots = slice(2 * b, 2 * b + 2)
             nc.vector.tensor_tensor(
-                out=x2b[i][:, h, go].rearrange("p (c i) t -> p c t i", i=4),
-                in0=t2[i][:, 4 * go : 4 * go + 4, rs].rearrange("p t (c i) -> p c t i", i=4),
-                in1=s2[(i, go, h)][:].rearrange("p t (c i) -> p c t i", i=4),
-                op=ADD,
+                out=x1[i][:, two_slots, :], in0=leak1[i // 2][:, i % 2, two_slots, :], in1=product1[(i, b)][:], op=ADD
             )
 
-        def QX2(i, h0, h1):
-            if h0 == 0:
-                x2c_t = work.tile([P, 2, 2, P], U32, name="x2c_t", bufs=4, align_bytes=64)
-                x2s_t = work.tile([P, 2, 2, P], U8, name="x2s_t", bufs=4, align_bytes=64)
-                x2c[i], x2s[i] = x2c_t, x2s_t
-            nc.vector.quantize_mx(
-                out=x2c[i][:, h0:h1].rearrange("p h g r -> p (h g r)").bitcast(FP8X4),
-                scales=x2s[i][:, h0:h1].rearrange("p h g r -> p (h g r)"),
-                in_=x2b[i][:, h0:h1].rearrange("p h g r t -> p (h g r t)"),
+        def interleave_x1(i):
+            x1_mixed_chunk = stream.tile([P, 2, ROWS, SLOTS], BF16, name="x1_mixed_chunk", align_bytes=64)
+            x1_mixed[i] = x1_mixed_chunk
+            for h in range(2):
+                mixed, by_slot = blocks_of_four(x1_mixed_chunk[:, h], x1[i][:, SLOTS * h : SLOTS * (h + 1), :])
+                nc.scalar.copy(out=mixed, in_=by_slot)
+
+        def quantize_x1(i):
+            x1_codes = stream.tile([P, 2, ROWS], U32, name="x1_codes", align_bytes=64)
+            x1_scales = stream.tile([P, 2, ROWS], U8, name="x1_scales", align_bytes=64)
+            x1_q[i] = (x1_codes, x1_scales)
+            quantize(
+                x1_codes[:].rearrange("p g r -> p (g r)"),
+                x1_scales[:].rearrange("p g r -> p (g r)"),
+                x1_mixed[i][:].rearrange("p g r t -> p (g r t)"),
             )
 
-        def S3(i, h, parts=1):
-            wd = R // parts
-            for q in range(parts):
-                yp = ps_y.tile([P, wd], F32, name="yp")
-                for g in range(2):
-                    nc.tensor.matmul_mx(
-                        out=yp[:],
-                        lhsT=x2c[i][:, h, g, :].bitcast(FP8X4),
-                        lhsT_scale=x2s[i][:, h, g, :],
-                        rhs=cc[0][:, g, q * wd : q * wd + wd].bitcast(FP8X4),
-                        rhs_scale=cs[0][:, g, q * wd : q * wd + wd],
-                        start=(g == 0),
-                        stop=(g == 1),
+
+        def leak_x1(i):
+            leak2_chunk = stream.tile([P, 2 * SLOTS, ROWS], F32, name="leak2_chunk")
+            leak2[i] = leak2_chunk
+            for n in range(2 * SLOTS):
+                if i >= LAST - 1 and n % 2 == 1:
+                    nc.vector.tensor_scalar(
+                        out=leak2_chunk[:, n, :],
+                        in0=x1[i][:, n, :],
+                        scalar1=column(a_f32, n),
+                        scalar2=column(d_f32, n),
+                        op0=MULT,
+                        op1=ADD,
                     )
-                y_ps[(i, h, q)] = yp
-
-        def YO(i, h, parts=1):
-            wd = R // parts
-            for q in range(parts):
-                y_sb = work.tile([P, wd], F32, name="y_sb" if parts == 1 else "y_half", bufs=6 if parts == 1 else 2)
-                if q == 0:
-                    nc.scalar.copy(out=y_sb[:], in_=y_ps[(i, h, q)][:])
                 else:
-                    nc.vector.tensor_copy(out=y_sb[:], in_=y_ps[(i, h, q)][:])
-                r0 = i * ROWS + h * P
-                eng = nc.sync if q == 0 else nc.scalar
-                eng.dma_start(out=out[r0 : r0 + P, q * wd : q * wd + wd], in_=y_sb[:])
+                    nc.scalar.activation(
+                        leak2_chunk[:, n, :], x1[i][:, n, :], IDENTITY, bias=column(d_f32, n), scale=column(a_f32, n)
+                    )
 
-        def WI(go, g, eng, t0=0, t1_=4):
-            if go not in wg:
-                wg_t = keep.tile([P, 2, 512, 4], BF16, name="wg%d" % go, align_bytes=64)
-                wg[go] = wg_t
-            o = wg[go][:, g].rearrange("p (t m) j -> p t m j", t=4)[:, t0:t1_]
-            i_ = w_raw[go][:, g].rearrange("p j (m t) -> p t m j", t=4)[:, t0:t1_]
-            if eng == "v":
-                nc.vector.tensor_copy(out=o, in_=i_)
-            else:
-                nc.scalar.copy(out=o, in_=i_)
+        def multiply2(i):
+            for r in range(2):
+                for h in range(2):
+                    bank = psum_step.tile([P, SLOTS, P], F32, name="bank_step")
+                    for t in range(SLOTS):
+                        multiply(
+                            bank[:, t, :],
+                            (w_codes[h], w_scales[h]),
+                            slice(t * P, (t + 1) * P),
+                            x1_q[i],
+                            slice(r * P, (r + 1) * P),
+                        )
+                    product2[(i, r, h)] = bank
 
-        def WQ(go):
-            wc_t = keep.tile([P, 2, 512], U32, name="wc%d" % go, align_bytes=64)
-            ws_t = keep.tile([P, 2, 512], U8, name="ws%d" % go, align_bytes=64)
-            wc[go], ws[go] = wc_t, ws_t
-            nc.vector.quantize_mx(
-                out=wc_t[:].rearrange("p g c -> p (g c)").bitcast(FP8X4),
-                scales=ws_t[:].rearrange("p g c -> p (g c)"),
-                in_=wg[go][:].rearrange("p g c j -> p (g c j)"),
+        def add2(i, r, h):
+            if (r, h) == (0, 0):
+                x2_mixed_chunk = stream.tile([P, 2, 2, P, SLOTS], BF16, name="x2_mixed_chunk", align_bytes=64)
+                x2_mixed[i] = x2_mixed_chunk
+            mixed, leak = blocks_of_four(
+                x2_mixed[i][:, r, h], leak2[i][:, SLOTS * h : SLOTS * (h + 1), r * P : (r + 1) * P]
+            )
+            nc.vector.tensor_tensor(
+                out=mixed, in0=leak, in1=product2[(i, r, h)][:].rearrange("p t (c i) -> p c t i", i=4), op=ADD
             )
 
-        def CW(g, j, eng):
-            if g not in cw:
-                cw_t = keep.tile([P, 4, R], BF16, name="cw%d" % g)
-                cw[g] = cw_t
-            i_ = c_by[:, g, j, :].bitcast(FP8)
-            if eng == "v":
-                nc.vector.tensor_scalar(out=cw[g][:, j, :], in0=i_, scalar1=c_sc[:, g, j : j + 1], scalar2=None, op0=MULT)
-            else:
-                nc.scalar.activation(cw[g][:, j, :], i_, mybir.ActivationFunctionType.Copy, scale=c_sc[:, g, j : j + 1])
-
-        def CI(g, eng="s"):
-            if 0 not in cg:
-                cg_t = keep.tile([P, 2, R, 4], BF16, name="cg", align_bytes=64)
-                cg[0] = cg_t
-            o = cg[0][:, g].rearrange("p (c i) j -> p c j i", i=4)
-            i_ = cw[g][:].rearrange("p j (c i) -> p c j i", i=4)
-            if eng == "s":
-                nc.scalar.copy(out=o, in_=i_)
-            else:
-                nc.vector.tensor_copy(out=o, in_=i_)
-
-        def CQ():
-            cc_t = keep.tile([P, 2, R], U32, name="cc", align_bytes=64)
-            cs_t = keep.tile([P, 2, R], U8, name="cs", align_bytes=64)
-            cc[0], cs[0] = cc_t, cs_t
-            nc.vector.quantize_mx(
-                out=cc_t[:].rearrange("p g r -> p (g r)").bitcast(FP8X4),
-                scales=cs_t[:].rearrange("p g r -> p (g r)"),
-                in_=cg[0][:].rearrange("p g r j -> p (g r j)"),
+        def quantize_x2(i, r0, r1):
+            if r0 == 0:
+                x2_codes = x2_pool.tile([P, 2, 2, P], U32, name="x2_codes", align_bytes=64)
+                x2_scales = x2_pool.tile([P, 2, 2, P], U8, name="x2_scales", align_bytes=64)
+                x2_q[i] = (x2_codes, x2_scales)
+            quantize(
+                x2_q[i][0][:, r0:r1].rearrange("p q g r -> p (q g r)"),
+                x2_q[i][1][:, r0:r1].rearrange("p q g r -> p (q g r)"),
+                x2_mixed[i][:, r0:r1].rearrange("p q g r t -> p (q g r t)"),
             )
+
+
+        def multiply_y(i, r, parts):
+            width = R // parts
+            for q in range(parts):
+                bank = psum_y.tile([P, width], F32, name="bank_y")
+                x2_tile = (x2_q[i][0][:, r], x2_q[i][1][:, r])
+                multiply(bank[:], x2_tile, slice(0, P), (c_codes, c_scales), slice(q * width, (q + 1) * width))
+                y_banks[(i, r, q)] = bank
+
+        def store_y(i, r, parts):
+            width = R // parts
+            for q in range(parts):
+                y = y_pool.tile([P, width], F32, name="y%d" % parts)
+                if q == 0:
+                    nc.scalar.copy(out=y[:], in_=y_banks[(i, r, q)][:])
+                else:
+                    nc.vector.tensor_copy(out=y[:], in_=y_banks[(i, r, q)][:])
+                queue = nc.sync if q == 0 else nc.scalar
+                row0 = i * ROWS + r * P
+                queue.dma_start(out=out[row0 : row0 + P, q * width : (q + 1) * width], in_=y[:])
 
         with tc.manual_schedule():
-            nc.scalar.dma_start(out=a_bf[:], in_=a.rearrange("(g p t) -> p g t", p=P, t=4))
-            nc.scalar.dma_start(out=d_bf[:], in_=d.rearrange("(g p t) -> p g t", p=P, t=4))
-            nc.vector.memset(warm[:], 0.0)
-            nc.scalar.activation(warm2[:], warm[:], IDENT)
-            make_identity(nc, ident[:])
+            nc.scalar.dma_start(out=a_bf16[:], in_=a.rearrange("(g p t) -> p g t", p=P, t=SLOTS))
+            nc.scalar.dma_start(out=d_bf16[:], in_=d.rearrange("(g p t) -> p g t", p=P, t=SLOTS))
+            nc.scalar.dma_start(out=c_scales_in[:], in_=c_scale.rearrange("(g p t) o -> p g (t o)", p=P, t=SLOTS))
+            nc.vector.memset(table_in[:], 0.0)
+            nc.scalar.activation(table_out[:], table_in[:], IDENTITY)
+            make_identity(nc, identity[:])
             load_x(0)
             load_w(0, 0)
             load_w(0, 1)
@@ -302,105 +310,95 @@ def tile_hopfield_euler_readout_t1_kernel(tc, x, w, a, d, c_bytes, c_scale, out)
             load_w(1, 1)
             load_x(2)
             load_x(3)
-            nc.sync.dma_start(out=c_by[:], in_=c_bytes.rearrange("(g p j) r -> p g j r", p=P, j=4))
-            nc.scalar.dma_start(out=c_sc[:], in_=c_scale.rearrange("(g p j) o -> p g (j o)", p=P, j=4))
-            for rt in range(4, 8):
-                load_x(rt)
-            nc.gpsimd.tensor_copy(out=a_f[:], in_=a_bf[:])
-            nc.gpsimd.tensor_copy(out=d_f[:], in_=d_bf[:])
+            load_c(0)
+            load_c(1)
+            for r in range(4, M // P):
+                load_x(r)
+            nc.gpsimd.tensor_copy(out=a_f32[:], in_=a_bf16[:])
+            nc.gpsimd.tensor_copy(out=d_f32[:], in_=d_bf16[:])
 
-            T(0)
-            XO(0)
-            WI(0, 0, "v")
-            WI(0, 1, "s", 2, 4)
-            WI(0, 1, "v", 0, 2)
-            T(1)
-            XO(1)
-            WQ(0)
-            QX(0)
-            S1(0, 0)
-            WI(1, 0, "v", 0, 2)
-            WI(1, 0, "s", 2, 4)
-            for n in range(4):
-                TMP1(0, n, "v")
-            for n in range(4, 8):
-                TMP1(0, n, "g")
-            WI(1, 1, "v", 0, 2)
-            WI(1, 1, "s", 2, 4)
-            WQ(1)
-            T(2)
-            T(3)
-            S1(0, 1)
-            XO(2)
-            XO(3)
-            A1(0, 0)
-            A1(0, 1)
-            QX(1)
-            for n in range(4):
-                TMP1(1, n, "g")
-            A1(0, 2)
-            A1(0, 3)
-            IL(0, 0)
-            IL(0, 1)
-            for n in range(4, 8):
-                TMP1(1, n)
-            for g in (0,):
-                for j in range(4):
-                    CW(g, j, "v")
-            for rt in range(4, 6):
-                T(rt)
-                XO(rt)
-            QX1(0)
+            turn_x(0)
+            copy_turned(0)
+            interleave_w(nc.vector.tensor_copy, 0, 0, slice(0, SLOTS))
+            share_interleave_w(0, 1)
+            turn_x(1)
+            copy_turned(1)
+            quantize_w(0)
+            quantize_x(0)
+            multiply1(0, 0)
+            share_interleave_w(1, 0)
+            share_interleave_w(1, 1)
+            for n in range(SLOTS):
+                leak_x(n % 2 == 1, 0, n, first=0, count=1)
+            quantize_w(1)
+            turn_x(2)
+            turn_x(3)
+            multiply1(0, 1)
+            copy_turned(2)
+            copy_turned(3)
+            add1(0, 0)
+            add1(0, 1)
+            quantize_x(1)
+            for n in range(SLOTS, 2 * SLOTS):
+                leak_x(True, 0, n, first=0, count=1)
+            add1(0, 2)
+            add1(0, 3)
+            interleave_x1(0)
+            for n in range(2 * SLOTS):
+                leak_x(False, 0, n, first=1, count=1)
+            for r in (4, 5):
+                turn_x(r)
+                copy_turned(r)
+            quantize_x1(0)
 
             for i in range(CHUNKS + 1):
-                if i < 2:
-                    for rt in (2 * i + 8, 2 * i + 9):
-                        load_x(rt)
-                if i + 1 < CHUNKS:
-                    S1(i + 1, 0)
-                    S1(i + 1, 1)
+                pair = i // 2 + 1
+                if i < LAST:
+                    multiply1(i + 1, 0)
+                    multiply1(i + 1, 1)
                 if i < CHUNKS:
-                    for n in range(8):
-                        TMP2(i, n)
-                for k in range(4):
-                    if i + 1 < CHUNKS:
-                        A1(i + 1, k)
-                        if i + 2 < CHUNKS:
-                            TMP1(i + 2, 2 * k)
-                            TMP1(i + 2, 2 * k + 1)
+                    leak_x1(i)
+                for b in range(4):
+                    if i in (1, 3) and b < 2:
+                        for n in (SLOTS + 2 * b, SLOTS + 2 * b + 1):
+                            leak_x(False, pair, n)
+                    if i < LAST:
+                        add1(i + 1, b)
                 if i < CHUNKS:
-                    S2(i)
-                if i + 1 < CHUNKS:
-                    IL(i + 1, 0)
-                    IL(i + 1, 1)
+                    multiply2(i)
+                if i < LAST:
+                    interleave_x1(i + 1)
                 if i == 3:
-                    CQ()
-                if i >= 3:
-                    for j in {3: (0, 1), 4: (2, 3), 5: (4,), 6: (5,)}[i]:
-                        last = j == CHUNKS - 1
-                        for h in range(2):
-                            S3(j, h, 2 if last and h else 1)
-                            YO(j, h, 2 if last and h else 1)
-                if i < 3:
-                    for rt in (2 * i + 6, 2 * i + 7):
-                        T(rt)
-                        XO(rt)
-                for k in range(4):
-                    if i < CHUNKS:
-                        A2(i, k)
-                        if k == 1 and i + 2 < CHUNKS:
-                            QX(i + 2)
-                        if i == CHUNKS - 1 and k == 2:
-                            QX2(i, 0, 1)
+                    quantize_c()
+                for chunk in READOUT_STEPS.get(i, ()):
+                    for r in range(2):
+                        parts = 2 if (chunk, r) == (LAST, 1) else 1
+                        multiply_y(chunk, r, parts)
+                        store_y(chunk, r, parts)
+                if i + 3 < CHUNKS:
+                    for r in (2 * i + 6, 2 * i + 7):
+                        turn_x(r)
+                        copy_turned(r)
+                if i < CHUNKS:
+                    add2(i, 0, 0)
+                    if i + 2 < CHUNKS:
+                        quantize_x(i + 2)
+                    add2(i, 0, 1)
+                    add2(i, 1, 0)
+                    if i == LAST:
+                        quantize_x2(i, 0, 1)
+                    add2(i, 1, 1)
+                if i == 1:
+                    widen_c(0)
                 if i == 2:
-                    for j in range(4):
-                        CW(1, j, "v")
-                if i == 2:
-                    CI(0)
-                    CI(1)
-                if i + 1 < CHUNKS:
-                    QX1(i + 1)
-                if i < CHUNKS - 1:
-                    QX2(i, 0, 2)
-                if i == CHUNKS - 1:
-                    QX2(i, 1, 2)
+                    widen_c(1)
+                    interleave_c(0)
+                    interleave_c(1)
+                if i in (0, 2):
+                    for n in range(SLOTS):
+                        leak_x(pair == 1, pair, n)
+                if i < LAST:
+                    quantize_x1(i + 1)
+                    quantize_x2(i, 0, 2)
+                if i == LAST:
+                    quantize_x2(i, 1, 2)

from contextlib import ExitStack

import concourse.mybir as mybir
from concourse.masks import make_identity

M, N, R = 1536, 1024, 512
FLOPS = 2 * M * N * (N + N + R)

P = 128
SLOTS = 4
HALF = P * SLOTS
ROWS = 256
CHUNKS = M // ROWS
LAST = CHUNKS - 1

F32 = mybir.dt.float32
BF16 = mybir.dt.bfloat16
U32 = mybir.dt.uint32
U8 = mybir.dt.uint8
FP8 = mybir.dt.float8_e4m3fn
FP8X4 = mybir.dt.float8_e4m3fn_x4
ADD = mybir.AluOpType.add
MULT = mybir.AluOpType.mult
COPY = mybir.ActivationFunctionType.Copy
IDENTITY = mybir.ActivationFunctionType.Identity

READOUT_STEPS = {3: (0, 1, 2), 4: (3,), 5: (4,), 6: (5,)}


def blocks_of_four(interleaved, by_slot):
    return (
        interleaved.rearrange("p (c i) t -> p c t i", i=4),
        by_slot.rearrange("p t (c i) -> p c t i", i=4),
    )


def tile_hopfield_euler_readout_t1_kernel(tc, x, w, a, d, c_bytes, c_scale, out):
    nc = tc.nc

    with ExitStack() as ctx:
        keep = ctx.enter_context(tc.tile_pool(name="keep", bufs=1))
        stream = ctx.enter_context(tc.tile_pool(name="stream", bufs=2))
        x_pool = ctx.enter_context(tc.tile_pool(name="x_pool", bufs=3))
        x2_pool = ctx.enter_context(tc.tile_pool(name="x2_pool", bufs=4))
        y_pool = ctx.enter_context(tc.tile_pool(name="y_pool", bufs=4))
        psum_step = ctx.enter_context(tc.psum_pool(name="psum_step", bufs=4))
        psum_turn = ctx.enter_context(tc.psum_pool(name="psum_turn", bufs=2))
        psum_y = ctx.enter_context(tc.psum_pool(name="psum_y", bufs=2))

        identity = keep.tile([P, P], F32)
        a_bf16 = keep.tile([P, 2, SLOTS], BF16)
        d_bf16 = keep.tile([P, 2, SLOTS], BF16)
        a_f32 = keep.tile([P, 2, SLOTS], F32)
        d_f32 = keep.tile([P, 2, SLOTS], F32)
        c_scales_in = keep.tile([P, 2, SLOTS], F32)
        c_bytes_in = keep.tile([P, 2, SLOTS, R], U8, align_bytes=64)
        c_wide = keep.tile([P, 2, SLOTS, R], BF16)
        c_mixed = keep.tile([P, 2, R, SLOTS], BF16, align_bytes=64)
        c_codes = keep.tile([P, 2, R], U32, align_bytes=64)
        c_scales = keep.tile([P, 2, R], U8, align_bytes=64)
        table_in = keep.tile([P, 1], F32)
        table_out = keep.tile([P, 1], F32)
        w_in, w_mixed, w_codes, w_scales = [], [], [], []
        for h in range(2):
            w_in.append(keep.tile([P, 2, SLOTS, HALF], BF16, name="w_in%d" % h))
            w_mixed.append(keep.tile([P, 2, HALF, SLOTS], BF16, name="w_mixed%d" % h, align_bytes=64))
            w_codes.append(keep.tile([P, 2, HALF], U32, name="w_codes%d" % h, align_bytes=64))
            w_scales.append(keep.tile([P, 2, HALF], U8, name="w_scales%d" % h, align_bytes=64))
        x_in = [keep.tile([P, N], BF16, name="x_in%d" % r) for r in range(M // P)]

        x_mixed, leak1, x1, x1_mixed, leak2, x2_mixed = {}, {}, {}, {}, {}, {}
        x_q, x1_q, x2_q = {}, {}, {}
        turned, product1, product2, y_banks = {}, {}, {}, {}

        def column(tile, n):
            return tile[:, n // SLOTS, n % SLOTS : n % SLOTS + 1]

        def quantize(out_codes, out_scales, values):
            nc.vector.quantize_mx(out=out_codes.bitcast(FP8X4), scales=out_scales, in_=values)

        def multiply(bank, stationary, stationary_cols, moving, moving_cols):
            for g in range(2):
                nc.tensor.matmul_mx(
                    out=bank,
                    lhsT=stationary[0][:, g, stationary_cols].bitcast(FP8X4),
                    lhsT_scale=stationary[1][:, g, stationary_cols],
                    rhs=moving[0][:, g, moving_cols].bitcast(FP8X4),
                    rhs_scale=moving[1][:, g, moving_cols],
                    start=(g == 0),
                    stop=(g == 1),
                )


        def load_w(h, g):
            rows = w[g * HALF : (g + 1) * HALF, h * HALF : (h + 1) * HALF]
            nc.sync.dma_start(out=w_in[h][:, g], in_=rows.rearrange("(p j) c -> p j c", j=SLOTS))

        def interleave_w(copy, h, g, slots):
            copy(
                out=w_mixed[h][:, g].rearrange("p (t m) j -> p t m j", t=SLOTS)[:, slots],
                in_=w_in[h][:, g].rearrange("p j (m t) -> p t m j", t=SLOTS)[:, slots],
            )

        def share_interleave_w(h, g):
            interleave_w(nc.vector.tensor_copy, h, g, slice(0, 2))
            interleave_w(nc.scalar.copy, h, g, slice(2, 4))

        def quantize_w(h):
            quantize(
                w_codes[h][:].rearrange("p g c -> p (g c)"),
                w_scales[h][:].rearrange("p g c -> p (g c)"),
                w_mixed[h][:].rearrange("p g c j -> p (g c j)"),
            )


        def load_c(g):
            rows = c_bytes[g * HALF : (g + 1) * HALF, :]
            nc.sync.dma_start(out=c_bytes_in[:, g], in_=rows.rearrange("(p j) r -> p j r", j=SLOTS))

        def widen_c(g):
            for j in range(SLOTS):
                values, scale = c_bytes_in[:, g, j, :].bitcast(FP8), c_scales_in[:, g, j : j + 1]
                if g == 0 and j < 2:
                    nc.scalar.activation(c_wide[:, g, j, :], values, COPY, scale=scale)
                else:
                    nc.vector.tensor_scalar(out=c_wide[:, g, j, :], in0=values, scalar1=scale, scalar2=None, op0=MULT)

        def interleave_c(g):
            mixed, by_slot = blocks_of_four(c_mixed[:, g], c_wide[:, g])
            nc.scalar.copy(out=mixed, in_=by_slot)

        def quantize_c():
            quantize(
                c_codes[:].rearrange("p g r -> p (g r)"),
                c_scales[:].rearrange("p g r -> p (g r)"),
                c_mixed[:].rearrange("p g r j -> p (g r j)"),
            )


        def load_x(r):
            nc.sync.dma_start(out=x_in[r][:], in_=x[r * P : (r + 1) * P, :])

        def turn_x(r):
            bank = psum_turn.tile([P, 2, 2, P], F32, name="bank_turned")
            words = x_in[r][:].bitcast(F32)
            for g in range(2):
                for u in range(2):
                    nc.tensor.transpose(bank[:, g, u, :], words[:, 256 * g + u : 256 * (g + 1) : 2], identity[:])
            turned[r] = bank

        def copy_turned(r):
            chunk, r0 = r // 2, (r % 2) * P
            if r % 4 == 0:
                x_mixed_pair = stream.tile([P, 2, 2, ROWS, 2], F32, name="x_mixed_pair", align_bytes=64)
                x_mixed[chunk // 2] = x_mixed_pair
            nc.scalar.copy(
                out=x_mixed[chunk // 2][:, chunk % 2, :, r0 : r0 + P, :],
                in_=turned[r][:].rearrange("p g u r -> p g r u"),
            )

        def quantize_x(i):
            x_codes = x_pool.tile([P, 2, ROWS], U32, name="x_codes", align_bytes=64)
            x_scales = x_pool.tile([P, 2, ROWS], U8, name="x_scales", align_bytes=64)
            x_q[i] = (x_codes, x_scales)
            quantize(
                x_codes[:].rearrange("p g r -> p (g r)"),
                x_scales[:].rearrange("p g r -> p (g r)"),
                x_mixed[i // 2][:, i % 2].rearrange("p g r u -> p (g r u)").bitcast(BF16),
            )


        def leak_x(on_scalar, pair, n, first=0, count=2):
            if pair not in leak1:
                leak1_pair = stream.tile([P, 2, 2 * SLOTS, ROWS], F32, name="leak1_pair")
                leak1[pair] = leak1_pair
            chunks = slice(first, first + count)
            values = x_mixed[pair][:].rearrange("p c g r u -> p (c g r u)").bitcast(BF16)
            values = values.rearrange("p (c g r t) -> p c g r t", c=2, g=2, t=SLOTS)
            values = values[:, chunks, n // SLOTS, :, n % SLOTS]
            leak = leak1[pair][:, chunks, n, :]
            if on_scalar:
                nc.scalar.activation(leak, values, IDENTITY, bias=column(d_f32, n), scale=column(a_f32, n))
            else:
                nc.vector.tensor_scalar(
                    out=leak, in0=values, scalar1=column(a_f32, n), scalar2=column(d_f32, n), op0=MULT, op1=ADD
                )

        def multiply1(i, h):
            for b in range(2):
                bank = psum_step.tile([P, 2, ROWS], F32, name="bank_step")
                for s in range(2):
                    t = 2 * b + s
                    multiply(bank[:, s, :], (w_codes[h], w_scales[h]), slice(t * P, (t + 1) * P), x_q[i], slice(0, ROWS))
                product1[(i, 2 * h + b)] = bank

        def add1(i, b):
            if b == 0:
                x1_chunk = stream.tile([P, 2 * SLOTS, ROWS], F32, name="x1_chunk")
                x1[i] = x1_chunk
            two_slots = slice(2 * b, 2 * b + 2)
            nc.vector.tensor_tensor(
                out=x1[i][:, two_slots, :], in0=leak1[i // 2][:, i % 2, two_slots, :], in1=product1[(i, b)][:], op=ADD
            )

        def interleave_x1(i):
            x1_mixed_chunk = stream.tile([P, 2, ROWS, SLOTS], BF16, name="x1_mixed_chunk", align_bytes=64)
            x1_mixed[i] = x1_mixed_chunk
            for h in range(2):
                mixed, by_slot = blocks_of_four(x1_mixed_chunk[:, h], x1[i][:, SLOTS * h : SLOTS * (h + 1), :])
                nc.scalar.copy(out=mixed, in_=by_slot)

        def quantize_x1(i):
            x1_codes = stream.tile([P, 2, ROWS], U32, name="x1_codes", align_bytes=64)
            x1_scales = stream.tile([P, 2, ROWS], U8, name="x1_scales", align_bytes=64)
            x1_q[i] = (x1_codes, x1_scales)
            quantize(
                x1_codes[:].rearrange("p g r -> p (g r)"),
                x1_scales[:].rearrange("p g r -> p (g r)"),
                x1_mixed[i][:].rearrange("p g r t -> p (g r t)"),
            )


        def leak_x1(i):
            leak2_chunk = stream.tile([P, 2 * SLOTS, ROWS], F32, name="leak2_chunk")
            leak2[i] = leak2_chunk
            for n in range(2 * SLOTS):
                if i >= LAST - 1 and n % 2 == 1:
                    nc.vector.tensor_scalar(
                        out=leak2_chunk[:, n, :],
                        in0=x1[i][:, n, :],
                        scalar1=column(a_f32, n),
                        scalar2=column(d_f32, n),
                        op0=MULT,
                        op1=ADD,
                    )
                else:
                    nc.scalar.activation(
                        leak2_chunk[:, n, :], x1[i][:, n, :], IDENTITY, bias=column(d_f32, n), scale=column(a_f32, n)
                    )

        def multiply2(i):
            for r in range(2):
                for h in range(2):
                    bank = psum_step.tile([P, SLOTS, P], F32, name="bank_step")
                    for t in range(SLOTS):
                        multiply(
                            bank[:, t, :],
                            (w_codes[h], w_scales[h]),
                            slice(t * P, (t + 1) * P),
                            x1_q[i],
                            slice(r * P, (r + 1) * P),
                        )
                    product2[(i, r, h)] = bank

        def add2(i, r, h):
            if (r, h) == (0, 0):
                x2_mixed_chunk = stream.tile([P, 2, 2, P, SLOTS], BF16, name="x2_mixed_chunk", align_bytes=64)
                x2_mixed[i] = x2_mixed_chunk
            mixed, leak = blocks_of_four(
                x2_mixed[i][:, r, h], leak2[i][:, SLOTS * h : SLOTS * (h + 1), r * P : (r + 1) * P]
            )
            nc.vector.tensor_tensor(
                out=mixed, in0=leak, in1=product2[(i, r, h)][:].rearrange("p t (c i) -> p c t i", i=4), op=ADD
            )

        def quantize_x2(i, r0, r1):
            if r0 == 0:
                x2_codes = x2_pool.tile([P, 2, 2, P], U32, name="x2_codes", align_bytes=64)
                x2_scales = x2_pool.tile([P, 2, 2, P], U8, name="x2_scales", align_bytes=64)
                x2_q[i] = (x2_codes, x2_scales)
            quantize(
                x2_q[i][0][:, r0:r1].rearrange("p q g r -> p (q g r)"),
                x2_q[i][1][:, r0:r1].rearrange("p q g r -> p (q g r)"),
                x2_mixed[i][:, r0:r1].rearrange("p q g r t -> p (q g r t)"),
            )


        def multiply_y(i, r, parts):
            width = R // parts
            for q in range(parts):
                bank = psum_y.tile([P, width], F32, name="bank_y")
                x2_tile = (x2_q[i][0][:, r], x2_q[i][1][:, r])
                multiply(bank[:], x2_tile, slice(0, P), (c_codes, c_scales), slice(q * width, (q + 1) * width))
                y_banks[(i, r, q)] = bank

        def store_y(i, r, parts):
            width = R // parts
            for q in range(parts):
                y = y_pool.tile([P, width], F32, name="y%d" % parts)
                if q == 0:
                    nc.scalar.copy(out=y[:], in_=y_banks[(i, r, q)][:])
                else:
                    nc.vector.tensor_copy(out=y[:], in_=y_banks[(i, r, q)][:])
                queue = nc.sync if q == 0 else nc.scalar
                row0 = i * ROWS + r * P
                queue.dma_start(out=out[row0 : row0 + P, q * width : (q + 1) * width], in_=y[:])

        with tc.manual_schedule():
            nc.scalar.dma_start(out=a_bf16[:], in_=a.rearrange("(g p t) -> p g t", p=P, t=SLOTS))
            nc.scalar.dma_start(out=d_bf16[:], in_=d.rearrange("(g p t) -> p g t", p=P, t=SLOTS))
            nc.scalar.dma_start(out=c_scales_in[:], in_=c_scale.rearrange("(g p t) o -> p g (t o)", p=P, t=SLOTS))
            nc.vector.memset(table_in[:], 0.0)
            nc.scalar.activation(table_out[:], table_in[:], IDENTITY)
            make_identity(nc, identity[:])
            load_x(0)
            load_w(0, 0)
            load_w(0, 1)
            load_x(1)
            load_w(1, 0)
            load_w(1, 1)
            load_x(2)
            load_x(3)
            load_c(0)
            load_c(1)
            for r in range(4, M // P):
                load_x(r)
            nc.gpsimd.tensor_copy(out=a_f32[:], in_=a_bf16[:])
            nc.gpsimd.tensor_copy(out=d_f32[:], in_=d_bf16[:])

            turn_x(0)
            copy_turned(0)
            interleave_w(nc.vector.tensor_copy, 0, 0, slice(0, SLOTS))
            share_interleave_w(0, 1)
            turn_x(1)
            copy_turned(1)
            quantize_w(0)
            quantize_x(0)
            multiply1(0, 0)
            share_interleave_w(1, 0)
            share_interleave_w(1, 1)
            for n in range(SLOTS):
                leak_x(n % 2 == 1, 0, n, first=0, count=1)
            quantize_w(1)
            turn_x(2)
            turn_x(3)
            multiply1(0, 1)
            copy_turned(2)
            copy_turned(3)
            add1(0, 0)
            add1(0, 1)
            quantize_x(1)
            for n in range(SLOTS, 2 * SLOTS):
                leak_x(True, 0, n, first=0, count=1)
            add1(0, 2)
            add1(0, 3)
            interleave_x1(0)
            for n in range(2 * SLOTS):
                leak_x(False, 0, n, first=1, count=1)
            for r in (4, 5):
                turn_x(r)
                copy_turned(r)
            quantize_x1(0)

            for i in range(CHUNKS + 1):
                pair = i // 2 + 1
                if i < LAST:
                    multiply1(i + 1, 0)
                    multiply1(i + 1, 1)
                if i < CHUNKS:
                    leak_x1(i)
                for b in range(4):
                    if i in (1, 3) and b < 2:
                        for n in (SLOTS + 2 * b, SLOTS + 2 * b + 1):
                            leak_x(False, pair, n)
                    if i < LAST:
                        add1(i + 1, b)
                if i < CHUNKS:
                    multiply2(i)
                if i < LAST:
                    interleave_x1(i + 1)
                if i == 3:
                    quantize_c()
                for chunk in READOUT_STEPS.get(i, ()):
                    for r in range(2):
                        parts = 2 if (chunk, r) == (LAST, 1) else 1
                        multiply_y(chunk, r, parts)
                        store_y(chunk, r, parts)
                if i + 3 < CHUNKS:
                    for r in (2 * i + 6, 2 * i + 7):
                        turn_x(r)
                        copy_turned(r)
                if i < CHUNKS:
                    add2(i, 0, 0)
                    if i + 2 < CHUNKS:
                        quantize_x(i + 2)
                    add2(i, 0, 1)
                    add2(i, 1, 0)
                    if i == LAST:
                        quantize_x2(i, 0, 1)
                    add2(i, 1, 1)
                if i == 1:
                    widen_c(0)
                if i == 2:
                    widen_c(1)
                    interleave_c(0)
                    interleave_c(1)
                if i in (0, 2):
                    for n in range(SLOTS):
                        leak_x(pair == 1, pair, n)
                if i < LAST:
                    quantize_x1(i + 1)
                    quantize_x2(i, 0, 2)
                if i == LAST:
                    quantize_x2(i, 1, 2)
